import numpy as np
import ml_dtypes


def mxq(x, axis, fmt="e4m3"):
    dtype, down = {"e4m3": (ml_dtypes.float8_e4m3fn, 7), "e5m2": (ml_dtypes.float8_e5m2, 14)}[fmt]
    v = np.moveaxis(np.asarray(x, np.float32).astype(ml_dtypes.bfloat16).astype(np.float64), axis, -1)
    blocks = v.reshape(v.shape[:-1] + (-1, 32))
    amax = np.abs(blocks).max(-1, keepdims=True)
    byte = np.maximum(np.where(amax > 0, np.frexp(amax)[1] - 1 + 127, 0) - down, 1)
    scale = np.exp2(byte - 127.0)
    codes = (blocks / scale).astype(np.float32).astype(dtype).astype(np.float64)
    return np.moveaxis((codes * scale).reshape(v.shape), -1, axis)


WIDE = False


def mx_kscale(k):
    if not WIDE:
        return np.ones(k)
    levels = np.array([10, -10, 5, -5, 0])
    if k % 512:
        return np.exp2(np.random.permutation(np.resize(levels, k // 32))).repeat(32)
    a = np.empty((k // 512, 16))
    for p in range(k // 512):
        a[p, :8] = np.random.permutation(np.resize(levels, 8))
        for g in range(8):
            far = levels[np.abs(levels - a[p, g]) >= 10]
            a[p, g + 8] = far[np.random.randint(len(far))]
    return np.exp2(a.ravel()).repeat(32)


def f64(x):
    return np.asarray(x).astype(np.float64)


def striped(idx):
    return np.tile(idx.reshape(-1, 16).T, (8, 1)).astype(np.uint16)


def unstriped(offs):
    return offs[:16].T.reshape(-1).astype(np.int64)


E2M1 = np.array([0.0, 0.5, 1.0, 1.5, 2.0, 3.0, 4.0, 6.0, -0.0, -0.5, -1.0, -1.5, -2.0, -3.0, -4.0, -6.0])


def pack_weight(w, fmt):
    k, n = w.shape
    w = f64(np.asarray(w, np.float32).astype(ml_dtypes.bfloat16)).reshape(k // 32, 32, n)
    amax = np.abs(w).max(1)
    if fmt == "e4m3":
        byte = np.frexp(amax)[1] - 1 + 127 - 7
    else:
        mant, ex = np.frexp(amax / 6.0)
        byte = np.where(mant > 0.5, ex, ex - 1) + 127
    byte = np.clip(np.where(amax > 0, byte, 1), 1, 254)
    scaled = (w * np.exp2(127.0 - byte)[:, None, :]).reshape(k, n).astype(np.float32)
    by_word = np.ascontiguousarray(scaled.reshape(k // 512, 128, 4, n).transpose(0, 1, 3, 2))
    if fmt == "e4m3":
        words = by_word.astype(ml_dtypes.float8_e4m3fn).view(np.uint8)
    else:
        c = by_word.astype(ml_dtypes.float4_e2m1fn).view(np.uint8) & 0xF
        words = (c[..., 0::2] | (c[..., 1::2] << 4)).reshape(k // 512, 128, 2 * n)
    return np.ascontiguousarray(words), np.ascontiguousarray(byte.astype(np.uint8).reshape(k // 512, 16, n))


def unpack_weight(words, scales, fmt):
    g, _, n = scales.shape
    words = np.ascontiguousarray(words).reshape(g, 128, n, -1)
    if fmt == "e4m3":
        vals = words.view(ml_dtypes.float8_e4m3fn).astype(np.float64)
    else:
        nib = np.empty((g, 128, n, 4), np.uint8)
        nib[..., 0::2] = words & 0xF
        nib[..., 1::2] = words >> 4
        vals = E2M1[nib]
    vals = vals * np.repeat(np.exp2(scales.astype(np.float64) - 127.0), 8, axis=1)[..., None]
    return vals.transpose(0, 1, 3, 2).reshape(g * 512, n)


def pack_table(v):
    words, scales = pack_weight(v, "e4m3")
    return np.concatenate([words.reshape(words.shape[0], -1), scales.reshape(scales.shape[0], -1)], axis=1)


def unpack_table(tab):
    g, t = tab.shape[0], tab.shape[1] // 528
    return unpack_weight(tab[:, :512 * t].reshape(g, 128, t, 4), tab[:, 512 * t:].reshape(g, 16, t), "e4m3")


def split(x):
    m, e = np.frexp(f64(x))
    hi = np.ldexp(np.trunc(16.0 * m) / 16.0, e)
    return hi, f64(x) - hi


K, M, T, S = 1024, 512, 1024, 512


def setup_inputs():
    n = np.random.standard_normal
    s = mx_kscale(K)[:, None]
    return {
        "tab": pack_table(n((K, T)) * s),
        "w": (n((K, M)) / np.sqrt(K) / s).astype(np.float32),
        "b": (0.3 * n(512)).astype(np.float32),
        "offs": striped(np.random.permutation(T)[:S]),
    }


def reference(tab, w, b, offs):
    tab_ = unpack_table(tab)[:, unstriped(offs)]
    w_hi, w_lo = split(w)
    w_hi_, w_lo_ = mxq(w_hi, 0, "e4m3"), mxq(w_lo, 0, "e4m3")
    y = w_hi_.T @ tab_ + w_lo_.T @ tab_
    return y + f64(b)[:, None]

@@ -1,0 +1,199 @@
+import concourse.mybir as mybir
+
+K, M, T, S = 1024, 512, 1024, 512
+FLOPS = 2 * 2 * K * M * S
+
+F32 = mybir.dt.float32
+BF16 = mybir.dt.bfloat16
+I32 = mybir.dt.int32
+U32 = mybir.dt.uint32
+U16 = mybir.dt.uint16
+U8 = mybir.dt.uint8
+FP8X4 = mybir.dt.float8_e4m3fn_x4
+ALU = mybir.AluOpType
+ACT = mybir.ActivationFunctionType
+
+P = 128
+PACK = 4
+K_PASS = P * PACK
+MASK = -983056
+
+
+def tile_list_tabw_hl_bias_kernel(tc, tab, w, b, offs, out):
+    nc = tc.nc
+    with (
+        tc.tile_pool(name="keep", bufs=1) as keep,
+        tc.psum_pool(name="psum", bufs=1) as psum,
+    ):
+        offsets = keep.tile([P, S // 16], U16, name="offsets")
+        planes = keep.tile([P, T // 4], I32, name="planes", align_bytes=64)
+        bias = keep.tile([P, M // P], F32, name="bias")
+        dummy = keep.tile([P, 1], F32, name="dummy")
+        nc.gpsimd.memset(planes[:], 0)
+        nc.vector.memset(dummy[:], 0.0)
+        nc.scalar.activation(dummy[:], dummy[:], ACT.Identity)
+
+        units = [(0, 0, 256), (1, 0, 256), (0, 256, 256), (1, 256, 256)]
+        w_sb, top, hl, codes, scales = [], [], [], [], []
+        for u, (a, c, n) in enumerate(units):
+            w_sb.append(keep.tile([P, PACK, n], F32, name="w_sb%d" % u, align_bytes=64))
+            top.append(keep.tile([P, n, PACK], BF16, name="top%d" % u, align_bytes=64))
+            hl.append(keep.tile([P, 2, n, PACK], BF16, name="hl%d" % u, align_bytes=64))
+            codes.append(keep.tile([P, 2, n], U32, name="codes%d" % u, align_bytes=64))
+            scales.append(keep.tile([P, 2, n], U8, name="scales%d" % u, align_bytes=64))
+        words = [keep.tile([P, T], I32, name="words%d" % a, align_bytes=64) for a in range(2)]
+        picked = [keep.tile([P, S], U32, name="picked%d" % a, align_bytes=64) for a in range(2)]
+        picked_scales = keep.tile([P, S], U8, name="picked_scales", align_bytes=64)
+
+        def load_w(u):
+            a, c, n = units[u]
+            nc.sync.dma_start(
+                out=w_sb[u][:],
+                in_=w[a * K_PASS : (a + 1) * K_PASS, c : c + n].rearrange("(p j) n -> p j n", j=PACK),
+            )
+
+        def load_table(a):
+            nc.sync.dma_start(
+                out=words[a][:],
+                in_=tab[a, 0 : 4 * P * T].rearrange("(p x) -> p x", p=P).bitcast(I32),
+            )
+
+        def load_offsets():
+            nc.sync.dma_start(offsets[:], offs)
+
+        def load_rows():
+            for q in range(4):
+                lo = 4 * P * T + 4 * q * T
+                nc.sync.dma_start(
+                    out=planes[32 * q : 32 * q + 8, :],
+                    in_=tab[:, lo : lo + 4 * T].rearrange("a (r t) -> a r t", r=4).bitcast(I32),
+                )
+
+        def load_bias():
+            with nc.allow_non_contiguous_dma(reason="512 bias values, one to a partition and column"):
+                nc.sync.dma_start(out=bias[:], in_=b.rearrange("(m p) -> p m", p=P))
+
+        def take_top(u, c0, n):
+            upper = w_sb[u][:, :, c0 : c0 + n].bitcast(BF16).rearrange("p j (c i e) -> p c j i e", i=4, e=2)[:, :, :, :, 1]
+            nc.scalar.copy(out=top[u][:, c0 : c0 + n].rearrange("p (c i) j -> p c j i", i=4), in_=upper)
+
+        def mask(u, c0, n):
+            nc.vector.tensor_scalar(
+                hl[u][:, 0, c0 : c0 + n].rearrange("p n j -> p (n j)").bitcast(I32),
+                top[u][:, c0 : c0 + n].rearrange("p n j -> p (n j)").bitcast(I32),
+                MASK,
+                None,
+                op0=ALU.bitwise_and,
+            )
+
+        def rest(u, c0, n, engine=nc.vector):
+            engine.tensor_tensor(
+                out=hl[u][:, 1, c0 : c0 + n].rearrange("p (c i) j -> p c j i", i=4),
+                in0=w_sb[u][:, :, c0 : c0 + n].rearrange("p j (c i) -> p c j i", i=4),
+                in1=hl[u][:, 0, c0 : c0 + n].rearrange("p (c i) j -> p c j i", i=4),
+                op=ALU.subtract,
+            )
+
+        def quantize_both(u):
+            nc.vector.quantize_mx(
+                out=codes[u][:].rearrange("p s n -> p (s n)").bitcast(FP8X4),
+                scales=scales[u][:].rearrange("p s n -> p (s n)"),
+                in_=hl[u][:].rearrange("p s n j -> p (s n j)"),
+            )
+
+        def quantize_part(u, s, c0, n):
+            nc.vector.quantize_mx(
+                out=codes[u][:, s, c0 : c0 + n].bitcast(FP8X4),
+                scales=scales[u][:, s, c0 : c0 + n],
+                in_=hl[u][:, s, c0 : c0 + n].rearrange("p n j -> p (n j)"),
+            )
+
+        def gather_words(a):
+            nc.vector.tensor_copy(picked[a][:], words[a][:].bitcast(U32).indirect(offsets[:]))
+
+        def gather_scales():
+            nc.vector.tensor_copy(picked_scales[:], planes[:].bitcast(U8).indirect(offsets[:]))
+
+        banks = {}
+        for m in range(4):
+            halves = [(0, 512)] if m < 2 else [(0, 256), (256, 256)]
+            banks[m] = [(j0, jn, psum.tile([P, 512], F32, name="acc%d_%d" % (m, j0))) for j0, jn in halves]
+
+        def multiply(u, part, m):
+            a, c, n = units[u]
+            cols = slice(m * P - c, m * P - c + P)
+            for j0, jn, acc in banks[m]:
+                nc.tensor.matmul_mx(
+                    out=acc[:, 0:jn],
+                    lhsT=codes[u][:, part, cols].bitcast(FP8X4),
+                    lhsT_scale=scales[u][:, part, cols],
+                    rhs=picked[a][:, j0 : j0 + jn].bitcast(FP8X4),
+                    rhs_scale=picked_scales[4 * a : P, j0 : j0 + jn],
+                    start=(a == 0 and part == 0),
+                    stop=(a == 1 and part == 1),
+                )
+
+        def finish(m, h, engine):
+            j0, jn, acc = banks[m][h]
+            res = keep.tile([P, jn], F32, name="res%d_%d" % (m, j0), align_bytes=64)
+            if engine == "scalar":
+                nc.scalar.activation(res[:], acc[:, 0:jn], ACT.Identity, bias=bias[:, m : m + 1])
+            else:
+                nc.vector.tensor_scalar(res[:], acc[:, 0:jn], bias[:, m : m + 1], None, op0=ALU.add)
+            nc.sync.dma_start(out=out[m * P : (m + 1) * P, j0 : j0 + jn], in_=res[:])
+
+        load_table(0)
+        load_offsets()
+        load_table(1)
+        load_rows()
+        load_w(0)
+        load_w(1)
+        load_w(2)
+        load_w(3)
+        load_bias()
+        take_top(0, 0, 128)
+        take_top(0, 128, 128)
+        take_top(1, 0, 128)
+        take_top(1, 128, 128)
+        take_top(2, 0, 256)
+        take_top(3, 0, 256)
+        gather_words(0)
+        gather_words(1)
+        gather_scales()
+        mask(0, 0, 256)
+        rest(0, 0, 256)
+        mask(1, 0, 256)
+        quantize_both(0)
+        multiply(0, 0, 0)
+        multiply(0, 1, 0)
+        multiply(0, 0, 1)
+        multiply(0, 1, 1)
+        rest(1, 0, 256)
+        mask(2, 0, 256)
+        quantize_both(1)
+        multiply(1, 0, 0)
+        multiply(1, 1, 0)
+        finish(0, 0, "scalar")
+        multiply(1, 0, 1)
+        multiply(1, 1, 1)
+        finish(1, 0, "scalar")
+        rest(2, 0, 256)
+        mask(3, 0, 256)
+        quantize_both(2)
+        multiply(2, 0, 2)
+        multiply(2, 1, 2)
+        multiply(2, 0, 3)
+        multiply(2, 1, 3)
+        rest(3, 0, 128)
+        quantize_part(3, 0, 0, 256)
+        multiply(3, 0, 2)
+        multiply(3, 0, 3)
+        rest(3, 128, 128)
+        quantize_part(3, 1, 0, 128)
+        multiply(3, 1, 2)
+        quantize_part(3, 1, 128, 128)
+        multiply(3, 1, 3)
+        finish(2, 0, "vector")
+        finish(2, 1, "scalar")
+        finish(3, 0, "vector")
+        finish(3, 1, "scalar")

@@ -17,6 +17,8 @@ P = 128
 PACK = 4
 K_PASS = P * PACK
 MASK = -983056
+TOP_I = 4
+REST_I = 4
 
 
 def tile_list_tabw_hl_bias_kernel(tc, tab, w, b, offs, out):
@@ -33,33 +35,33 @@ def tile_list_tabw_hl_bias_kernel(tc, tab, w, b, offs, out):
         nc.vector.memset(dummy[:], 0.0)
         nc.scalar.activation(dummy[:], dummy[:], ACT.Identity)
 
-        units = [(0, 0, 256), (1, 0, 256), (0, 256, 256), (1, 256, 256)]
-        w_sb, top, hl, codes, scales = [], [], [], [], []
-        for u, (a, c, n) in enumerate(units):
-            w_sb.append(keep.tile([P, PACK, n], F32, name="w_sb%d" % u, align_bytes=64))
-            top.append(keep.tile([P, n, PACK], BF16, name="top%d" % u, align_bytes=64))
-            hl.append(keep.tile([P, 2, n, PACK], BF16, name="hl%d" % u, align_bytes=64))
-            codes.append(keep.tile([P, 2, n], U32, name="codes%d" % u, align_bytes=64))
-            scales.append(keep.tile([P, 2, n], U8, name="scales%d" % u, align_bytes=64))
+        units = [[(0, 0), (0, 1)], [(1, 0), (1, 1)], [(0, 2), (1, 2)], [(0, 3), (1, 3)]]
+        top, hl, codes, scales = [], [], [], []
+        for u in range(4):
+            top.append(keep.tile([P, 2 * P * PACK], BF16, name="top%d" % u, align_bytes=64))
+            hl.append(keep.tile([P, 4 * P * PACK], BF16, name="hl%d" % u, align_bytes=64))
+            codes.append(keep.tile([P, 4 * P], U32, name="codes%d" % u, align_bytes=64))
+            scales.append(keep.tile([P, 4 * P], U8, name="scales%d" % u, align_bytes=64))
         words = [keep.tile([P, T], I32, name="words%d" % a, align_bytes=64) for a in range(2)]
         picked = [keep.tile([P, S], U32, name="picked%d" % a, align_bytes=64) for a in range(2)]
         picked_scales = keep.tile([P, S], U8, name="picked_scales", align_bytes=64)
+        w_sb = {}
 
-        def load_w(u):
-            a, c, n = units[u]
+        def load_w(a, m, tiles):
+            n = tiles * P
+            piece = keep.tile([P, PACK, n], F32, name="w%d_%d" % (a, m), align_bytes=64)
             nc.sync.dma_start(
-                out=w_sb[u][:],
-                in_=w[a * K_PASS : (a + 1) * K_PASS, c : c + n].rearrange("(p j) n -> p j n", j=PACK),
+                out=piece[:],
+                in_=w[a * K_PASS : (a + 1) * K_PASS, m * P : m * P + n].rearrange("(p j) n -> p j n", j=PACK),
             )
+            for i in range(tiles):
+                w_sb[(a, m + i)] = (piece, i * P)
 
         def load_table(a):
             nc.sync.dma_start(
                 out=words[a][:],
                 in_=tab[a, 0 : 4 * P * T].rearrange("(p x) -> p x", p=P).bitcast(I32),
             )
-
-        def load_offsets():
-            nc.sync.dma_start(offsets[:], offs)
 
         def load_rows():
             for q in range(4):
@@ -73,39 +75,40 @@ def tile_list_tabw_hl_bias_kernel(tc, tab, w, b, offs, out):
             with nc.allow_non_contiguous_dma(reason="512 bias values, one to a partition and column"):
                 nc.sync.dma_start(out=bias[:], in_=b.rearrange("(m p) -> p m", p=P))
 
-        def take_top(u, c0, n):
-            upper = w_sb[u][:, :, c0 : c0 + n].bitcast(BF16).rearrange("p j (c i e) -> p c j i e", i=4, e=2)[:, :, :, :, 1]
-            nc.scalar.copy(out=top[u][:, c0 : c0 + n].rearrange("p (c i) j -> p c j i", i=4), in_=upper)
+        def source(u, h, halves):
+            piece, c = w_sb[units[u][h]]
+            return piece[:, :, c : c + halves * P]
 
-        def mask(u, c0, n):
+        def span(first, count):
+            return slice(first * P * PACK, (first + count) * P * PACK)
+
+        def take_top(u, h, halves):
+            upper = source(u, h, halves).bitcast(BF16).rearrange("p j (c i e) -> p c j i e", i=TOP_I, e=2)[:, :, :, :, 1]
+            nc.scalar.copy(out=top[u][:, span(h, halves)].rearrange("p (c i j) -> p c j i", i=TOP_I, j=PACK), in_=upper)
+
+        def mask(u, h, halves):
             nc.vector.tensor_scalar(
-                hl[u][:, 0, c0 : c0 + n].rearrange("p n j -> p (n j)").bitcast(I32),
-                top[u][:, c0 : c0 + n].rearrange("p n j -> p (n j)").bitcast(I32),
+                hl[u][:, span(h, halves)].bitcast(I32),
+                top[u][:, span(h, halves)].bitcast(I32),
                 MASK,
                 None,
                 op0=ALU.bitwise_and,
             )
 
-        def rest(u, c0, n, engine=nc.vector):
-            engine.tensor_tensor(
-                out=hl[u][:, 1, c0 : c0 + n].rearrange("p (c i) j -> p c j i", i=4),
-                in0=w_sb[u][:, :, c0 : c0 + n].rearrange("p j (c i) -> p c j i", i=4),
-                in1=hl[u][:, 0, c0 : c0 + n].rearrange("p (c i) j -> p c j i", i=4),
+        def rest(u, h, halves):
+            nc.vector.tensor_tensor(
+                out=hl[u][:, span(2 + h, halves)].rearrange("p (c i j) -> p c j i", i=REST_I, j=PACK),
+                in0=source(u, h, halves).rearrange("p j (c i) -> p c j i", i=REST_I),
+                in1=hl[u][:, span(h, halves)].rearrange("p (c i j) -> p c j i", i=REST_I, j=PACK),
                 op=ALU.subtract,
             )
 
-        def quantize_both(u):
+        def quantize(u, first, count):
+            cols = slice(first * P, (first + count) * P)
             nc.vector.quantize_mx(
-                out=codes[u][:].rearrange("p s n -> p (s n)").bitcast(FP8X4),
-                scales=scales[u][:].rearrange("p s n -> p (s n)"),
-                in_=hl[u][:].rearrange("p s n j -> p (s n j)"),
-            )
-
-        def quantize_part(u, s, c0, n):
-            nc.vector.quantize_mx(
-                out=codes[u][:, s, c0 : c0 + n].bitcast(FP8X4),
-                scales=scales[u][:, s, c0 : c0 + n],
-                in_=hl[u][:, s, c0 : c0 + n].rearrange("p n j -> p (n j)"),
+                out=codes[u][:, cols].bitcast(FP8X4),
+                scales=scales[u][:, cols],
+                in_=hl[u][:, span(first, count)],
             )
 
         def gather_words(a):
@@ -116,22 +119,24 @@ def tile_list_tabw_hl_bias_kernel(tc, tab, w, b, offs, out):
 
         banks = {}
         for m in range(4):
-            halves = [(0, 512)] if m < 2 else [(0, 256), (256, 256)]
-            banks[m] = [(j0, jn, psum.tile([P, 512], F32, name="acc%d_%d" % (m, j0))) for j0, jn in halves]
+            ranges = [(0, 512)] if m < 3 else [(0, 256), (256, 256)]
+            banks[m] = [(j0, jn, psum.tile([P, 512], F32, name="acc%d_%d" % (m, j0))) for j0, jn in ranges]
+        done = {m: 0 for m in range(4)}
 
-        def multiply(u, part, m):
-            a, c, n = units[u]
-            cols = slice(m * P - c, m * P - c + P)
+        def multiply(u, part, h):
+            a, m = units[u][h]
+            cols = slice((2 * part + h) * P, (2 * part + h + 1) * P)
             for j0, jn, acc in banks[m]:
                 nc.tensor.matmul_mx(
                     out=acc[:, 0:jn],
-                    lhsT=codes[u][:, part, cols].bitcast(FP8X4),
-                    lhsT_scale=scales[u][:, part, cols],
+                    lhsT=codes[u][:, cols].bitcast(FP8X4),
+                    lhsT_scale=scales[u][:, cols],
                     rhs=picked[a][:, j0 : j0 + jn].bitcast(FP8X4),
                     rhs_scale=picked_scales[4 * a : P, j0 : j0 + jn],
-                    start=(a == 0 and part == 0),
-                    stop=(a == 1 and part == 1),
+                    start=(done[m] == 0),
+                    stop=(done[m] == 3),
                 )
+            done[m] = done[m] + 1
 
         def finish(m, h, engine):
             j0, jn, acc = banks[m][h]
@@ -143,57 +148,64 @@ def tile_list_tabw_hl_bias_kernel(tc, tab, w, b, offs, out):
             nc.sync.dma_start(out=out[m * P : (m + 1) * P, j0 : j0 + jn], in_=res[:])
 
         load_table(0)
-        load_offsets()
-        load_table(1)
+        nc.sync.dma_start(offsets[:], offs)
         load_rows()
-        load_w(0)
-        load_w(1)
-        load_w(2)
-        load_w(3)
+        load_w(0, 0, 1)
+        load_w(0, 1, 1)
+        load_w(1, 0, 2)
+        load_table(1)
+        load_w(0, 2, 1)
+        load_w(1, 2, 1)
+        load_w(0, 3, 1)
+        load_w(1, 3, 1)
         load_bias()
-        take_top(0, 0, 128)
-        take_top(0, 128, 128)
-        take_top(1, 0, 128)
-        take_top(1, 128, 128)
-        take_top(2, 0, 256)
-        take_top(3, 0, 256)
+        take_top(0, 0, 1)
+        take_top(0, 1, 1)
+        take_top(1, 0, 1)
+        take_top(1, 1, 1)
+        take_top(2, 0, 1)
+        take_top(2, 1, 1)
+        take_top(3, 0, 1)
+        take_top(3, 1, 1)
         gather_words(0)
-        gather_words(1)
         gather_scales()
-        mask(0, 0, 256)
-        rest(0, 0, 256)
-        mask(1, 0, 256)
-        quantize_both(0)
+        mask(0, 0, 1)
+        rest(0, 0, 1)
+        mask(0, 1, 1)
+        rest(0, 1, 1)
+        mask(1, 0, 2)
+        quantize(0, 0, 4)
         multiply(0, 0, 0)
         multiply(0, 1, 0)
         multiply(0, 0, 1)
         multiply(0, 1, 1)
-        rest(1, 0, 256)
-        mask(2, 0, 256)
-        quantize_both(1)
+        rest(1, 0, 2)
+        gather_words(1)
+        mask(2, 0, 2)
+        quantize(1, 0, 4)
         multiply(1, 0, 0)
         multiply(1, 1, 0)
         finish(0, 0, "scalar")
         multiply(1, 0, 1)
         multiply(1, 1, 1)
         finish(1, 0, "scalar")
-        rest(2, 0, 256)
-        mask(3, 0, 256)
-        quantize_both(2)
-        multiply(2, 0, 2)
-        multiply(2, 1, 2)
-        multiply(2, 0, 3)
-        multiply(2, 1, 3)
-        rest(3, 0, 128)
-        quantize_part(3, 0, 0, 256)
-        multiply(3, 0, 2)
-        multiply(3, 0, 3)
-        rest(3, 128, 128)
-        quantize_part(3, 1, 0, 128)
-        multiply(3, 1, 2)
-        quantize_part(3, 1, 128, 128)
-        multiply(3, 1, 3)
-        finish(2, 0, "vector")
-        finish(2, 1, "scalar")
+        rest(2, 0, 1)
+        rest(2, 1, 1)
+        mask(3, 0, 2)
+        quantize(2, 0, 4)
+        multiply(2, 0, 0)
+        multiply(2, 0, 1)
+        multiply(2, 1, 0)
+        multiply(2, 1, 1)
+        finish(2, 0, "scalar")
+        rest(3, 0, 1)
+        quantize(3, 0, 2)
+        multiply(3, 0, 0)
+        multiply(3, 0, 1)
+        rest(3, 1, 1)
+        quantize(3, 2, 1)
+        multiply(3, 1, 0)
+        quantize(3, 3, 1)
+        multiply(3, 1, 1)
         finish(3, 0, "vector")
         finish(3, 1, "scalar")

@@ -36,6 +36,11 @@ def tile_list_tabw_hl_bias_kernel(tc, tab, w, b, offs, out):
         nc.scalar.activation(dummy[:], dummy[:], ACT.Identity)
 
         units = [[(0, 0), (0, 1)], [(1, 0), (1, 1)], [(0, 2), (1, 2)], [(0, 3), (1, 3)]]
+        by_half = [True, False, False, False]
+
+        def place(u, part, h):
+            return 2 * h + part if by_half[u] else 2 * part + h
+
         top, hl, codes, scales = [], [], [], []
         for u in range(4):
             top.append(keep.tile([P, 2 * P * PACK], BF16, name="top%d" % u, align_bytes=64))
@@ -88,7 +93,7 @@ def tile_list_tabw_hl_bias_kernel(tc, tab, w, b, offs, out):
 
         def mask(u, h, halves):
             nc.vector.tensor_scalar(
-                hl[u][:, span(h, halves)].bitcast(I32),
+                hl[u][:, span(place(u, 0, h), halves)].bitcast(I32),
                 top[u][:, span(h, halves)].bitcast(I32),
                 MASK,
                 None,
@@ -97,9 +102,9 @@ def tile_list_tabw_hl_bias_kernel(tc, tab, w, b, offs, out):
 
         def rest(u, h, halves):
             nc.vector.tensor_tensor(
-                out=hl[u][:, span(2 + h, halves)].rearrange("p (c i j) -> p c j i", i=REST_I, j=PACK),
+                out=hl[u][:, span(place(u, 1, h), halves)].rearrange("p (c i j) -> p c j i", i=REST_I, j=PACK),
                 in0=source(u, h, halves).rearrange("p j (c i) -> p c j i", i=REST_I),
-                in1=hl[u][:, span(h, halves)].rearrange("p (c i j) -> p c j i", i=REST_I, j=PACK),
+                in1=hl[u][:, span(place(u, 0, h), halves)].rearrange("p (c i j) -> p c j i", i=REST_I, j=PACK),
                 op=ALU.subtract,
             )
 
@@ -125,7 +130,7 @@ def tile_list_tabw_hl_bias_kernel(tc, tab, w, b, offs, out):
 
         def multiply(u, part, h):
             a, m = units[u][h]
-            cols = slice((2 * part + h) * P, (2 * part + h + 1) * P)
+            cols = slice(place(u, part, h) * P, (place(u, part, h) + 1) * P)
             for j0, jn, acc in banks[m]:
                 nc.tensor.matmul_mx(
                     out=acc[:, 0:jn],
@@ -172,14 +177,17 @@ def tile_list_tabw_hl_bias_kernel(tc, tab, w, b, offs, out):
         mask(0, 0, 1)
         rest(0, 0, 1)
         mask(0, 1, 1)
-        rest(0, 1, 1)
-        mask(1, 0, 2)
-        quantize(0, 0, 4)
+        quantize(0, 0, 2)
         multiply(0, 0, 0)
         multiply(0, 1, 0)
+        rest(0, 1, 1)
+        mask(1, 0, 1)
+        quantize(0, 2, 2)
         multiply(0, 0, 1)
         multiply(0, 1, 1)
-        rest(1, 0, 2)
+        mask(1, 1, 1)
+        rest(1, 0, 1)
+        rest(1, 1, 1)
         gather_words(1)
         mask(2, 0, 2)
         quantize(1, 0, 4)

@@ -1,4 +1,5 @@
 import concourse.mybir as mybir
+from concourse.masks import make_identity
 
 K, M, T, S = 1024, 512, 1024, 512
 FLOPS = 2 * 2 * K * M * S
@@ -76,9 +77,18 @@ def tile_list_tabw_hl_bias_kernel(tc, tab, w, b, offs, out):
                     in_=tab[:, lo : lo + 4 * T].rearrange("a (r t) -> a r t", r=4).bitcast(I32),
                 )
 
+        bias_rows = keep.tile([P, P], F32, name="bias_rows", align_bytes=64)
+        identity = keep.tile([P, P], F32, name="identity", align_bytes=64)
+        nc.gpsimd.memset(bias_rows[0 : P - M // P, :], 0.0)
+        make_identity(nc, identity[:])
+
         def load_bias():
-            with nc.allow_non_contiguous_dma(reason="512 bias values, one to a partition and column"):
-                nc.sync.dma_start(out=bias[:], in_=b.rearrange("(m p) -> p m", p=P))
+            nc.scalar.dma_start(out=bias_rows[P - M // P : P, :], in_=b.rearrange("(m p) -> m p", p=P))
+
+        def turn_bias():
+            turned = psum.tile([P, P], F32, name="turned")
+            nc.tensor.transpose(turned[:], bias_rows[:], identity[:])
+            nc.scalar.copy(out=bias[:], in_=turned[:, P - M // P : P])
 
         def source(u, h, halves):
             piece, c = w_sb[units[u][h]]
@@ -152,6 +162,8 @@ def tile_list_tabw_hl_bias_kernel(tc, tab, w, b, offs, out):
                 nc.vector.tensor_scalar(res[:], acc[:, 0:jn], bias[:, m : m + 1], None, op0=ALU.add)
             nc.sync.dma_start(out=out[m * P : (m + 1) * P, j0 : j0 + jn], in_=res[:])
 
+        load_bias()
+        turn_bias()
         load_table(0)
         nc.sync.dma_start(offsets[:], offs)
         load_rows()
@@ -163,7 +175,6 @@ def tile_list_tabw_hl_bias_kernel(tc, tab, w, b, offs, out):
         load_w(1, 2, 1)
         load_w(0, 3, 1)
         load_w(1, 3, 1)
-        load_bias()
         take_top(0, 0, 1)
         take_top(0, 1, 1)
         take_top(1, 0, 1)
@@ -186,23 +197,24 @@ def tile_list_tabw_hl_bias_kernel(tc, tab, w, b, offs, out):
         multiply(0, 0, 1)
         multiply(0, 1, 1)
         mask(1, 1, 1)
-        rest(1, 0, 1)
-        rest(1, 1, 1)
         gather_words(1)
-        mask(2, 0, 2)
-        quantize(1, 0, 4)
+        quantize(1, 0, 2)
         multiply(1, 0, 0)
+        multiply(1, 0, 1)
+        rest(1, 0, 2)
+        mask(2, 0, 2)
+        quantize(1, 2, 2)
         multiply(1, 1, 0)
         finish(0, 0, "scalar")
-        multiply(1, 0, 1)
         multiply(1, 1, 1)
         finish(1, 0, "scalar")
         rest(2, 0, 1)
-        rest(2, 1, 1)
-        mask(3, 0, 2)
-        quantize(2, 0, 4)
+        quantize(2, 0, 2)
         multiply(2, 0, 0)
         multiply(2, 0, 1)
+        rest(2, 1, 1)
+        mask(3, 0, 2)
+        quantize(2, 2, 2)
         multiply(2, 1, 0)
         multiply(2, 1, 1)
         finish(2, 0, "scalar")

@@ -17,9 +17,16 @@ ACT = mybir.ActivationFunctionType
 P = 128
 PACK = 4
 K_PASS = P * PACK
-MASK = -983056
-TOP_I = 4
-REST_I = 4
+PASSES = K // K_PASS
+TILES = M // P
+QUADRANT = 32
+SCALE_ROWS = 4
+HI_MASK = -983056
+TOP_RUN = 4
+REST_RUN = 2
+PIECES = [(0, 0), (0, 1), (1, 0), (1, 1), (0, 2), (1, 2), (0, 3), (1, 3)]
+FIRST_OF_PASS_1 = 2
+LOADED_BEFORE_TABLE_1 = 4
 
 
 def tile_list_tabw_hl_bias_kernel(tc, tab, w, b, offs, out):
@@ -30,100 +37,80 @@ def tile_list_tabw_hl_bias_kernel(tc, tab, w, b, offs, out):
     ):
         offsets = keep.tile([P, S // 16], U16, name="offsets")
         planes = keep.tile([P, T // 4], I32, name="planes", align_bytes=64)
-        bias = keep.tile([P, M // P], F32, name="bias")
-        dummy = keep.tile([P, 1], F32, name="dummy")
+        bias = keep.tile([P, TILES], F32, name="bias")
         nc.gpsimd.memset(planes[:], 0)
-        nc.vector.memset(dummy[:], 0.0)
-        nc.scalar.activation(dummy[:], dummy[:], ACT.Identity)
 
-        units = [[(0, 0), (0, 1)], [(1, 0), (1, 1)], [(0, 2), (1, 2)], [(0, 3), (1, 3)]]
-        by_half = [True, False, False, False]
-
-        def place(u, part, h):
-            return 2 * h + part if by_half[u] else 2 * part + h
-
-        top, hl, codes, scales = [], [], [], []
-        for u in range(4):
-            top.append(keep.tile([P, 2 * P * PACK], BF16, name="top%d" % u, align_bytes=64))
-            hl.append(keep.tile([P, 4 * P * PACK], BF16, name="hl%d" % u, align_bytes=64))
-            codes.append(keep.tile([P, 4 * P], U32, name="codes%d" % u, align_bytes=64))
-            scales.append(keep.tile([P, 4 * P], U8, name="scales%d" % u, align_bytes=64))
-        words = [keep.tile([P, T], I32, name="words%d" % a, align_bytes=64) for a in range(2)]
-        picked = [keep.tile([P, S], U32, name="picked%d" % a, align_bytes=64) for a in range(2)]
+        groups = 2 * len(PIECES)
+        top = keep.tile([P, len(PIECES) * P * PACK], BF16, name="top", align_bytes=64)
+        parts = keep.tile([P, groups * P * PACK], BF16, name="parts", align_bytes=64)
+        codes = keep.tile([P, groups * P], U32, name="codes", align_bytes=64)
+        scales = keep.tile([P, groups * P], U8, name="scales", align_bytes=64)
+        words = [keep.tile([P, T], I32, name="words%d" % a, align_bytes=64) for a in range(PASSES)]
+        picked = [keep.tile([P, S], U32, name="picked%d" % a, align_bytes=64) for a in range(PASSES)]
         picked_scales = keep.tile([P, S], U8, name="picked_scales", align_bytes=64)
-        w_sb = {}
+        w_sb = []
 
-        def load_w(a, m, tiles):
-            n = tiles * P
-            piece = keep.tile([P, PACK, n], F32, name="w%d_%d" % (a, m), align_bytes=64)
+        def load_w(i):
+            a, m = PIECES[i]
+            piece = keep.tile([P, PACK, P], F32, name="w%d_%d" % (a, m), align_bytes=64)
             nc.sync.dma_start(
                 out=piece[:],
-                in_=w[a * K_PASS : (a + 1) * K_PASS, m * P : m * P + n].rearrange("(p j) n -> p j n", j=PACK),
+                in_=w[a * K_PASS : (a + 1) * K_PASS, m * P : (m + 1) * P].rearrange("(p j) n -> p j n", j=PACK),
             )
-            for i in range(tiles):
-                w_sb[(a, m + i)] = (piece, i * P)
+            w_sb.append(piece)
 
         def load_table(a):
             nc.sync.dma_start(
                 out=words[a][:],
-                in_=tab[a, 0 : 4 * P * T].rearrange("(p x) -> p x", p=P).bitcast(I32),
+                in_=tab[a, 0 : PACK * P * T].rearrange("(p x) -> p x", p=P).bitcast(I32),
             )
 
-        def load_rows():
-            for q in range(4):
-                lo = 4 * P * T + 4 * q * T
+        def load_scale_rows():
+            for q in range(P // QUADRANT):
+                first = PACK * P * T + SCALE_ROWS * q * T
                 nc.sync.dma_start(
-                    out=planes[32 * q : 32 * q + 8, :],
-                    in_=tab[:, lo : lo + 4 * T].rearrange("a (r t) -> a r t", r=4).bitcast(I32),
+                    out=planes[QUADRANT * q : QUADRANT * q + PASSES * SCALE_ROWS, :],
+                    in_=tab[:, first : first + SCALE_ROWS * T].rearrange("a (r t) -> a r t", r=SCALE_ROWS).bitcast(I32),
                 )
 
         bias_rows = keep.tile([P, P], F32, name="bias_rows", align_bytes=64)
         identity = keep.tile([P, P], F32, name="identity", align_bytes=64)
-        nc.gpsimd.memset(bias_rows[0 : P - M // P, :], 0.0)
+        zero = keep.tile([P, 1], F32, name="zero")
+        nc.vector.memset(zero[:], 0.0)
+        spare = P - TILES
+        nc.scalar.activation(bias_rows[0:spare, :], zero[0:spare, :].to_broadcast([spare, P]), ACT.Identity)
         make_identity(nc, identity[:])
-
-        def load_bias():
-            nc.scalar.dma_start(out=bias_rows[P - M // P : P, :], in_=b.rearrange("(m p) -> m p", p=P))
-
-        def turn_bias():
-            turned = psum.tile([P, P], F32, name="turned")
-            nc.tensor.transpose(turned[:], bias_rows[:], identity[:])
-            nc.scalar.copy(out=bias[:], in_=turned[:, P - M // P : P])
-
-        def source(u, h, halves):
-            piece, c = w_sb[units[u][h]]
-            return piece[:, :, c : c + halves * P]
 
         def span(first, count):
             return slice(first * P * PACK, (first + count) * P * PACK)
 
-        def take_top(u, h, halves):
-            upper = source(u, h, halves).bitcast(BF16).rearrange("p j (c i e) -> p c j i e", i=TOP_I, e=2)[:, :, :, :, 1]
-            nc.scalar.copy(out=top[u][:, span(h, halves)].rearrange("p (c i j) -> p c j i", i=TOP_I, j=PACK), in_=upper)
+        def take_top(i):
+            upper = w_sb[i][:].bitcast(BF16).rearrange("p j (c i e) -> p c j i e", i=TOP_RUN, e=2)[:, :, :, :, 1]
+            nc.scalar.copy(out=top[:, span(i, 1)].rearrange("p (c i j) -> p c j i", i=TOP_RUN, j=PACK), in_=upper)
 
-        def mask(u, h, halves):
+        def mask(i):
             nc.vector.tensor_scalar(
-                hl[u][:, span(place(u, 0, h), halves)].bitcast(I32),
-                top[u][:, span(h, halves)].bitcast(I32),
-                MASK,
+                parts[:, span(2 * i, 1)].bitcast(I32),
+                top[:, span(i, 1)].bitcast(I32),
+                HI_MASK,
                 None,
                 op0=ALU.bitwise_and,
             )
 
-        def rest(u, h, halves):
+        def rest(i):
             nc.vector.tensor_tensor(
-                out=hl[u][:, span(place(u, 1, h), halves)].rearrange("p (c i j) -> p c j i", i=REST_I, j=PACK),
-                in0=source(u, h, halves).rearrange("p j (c i) -> p c j i", i=REST_I),
-                in1=hl[u][:, span(place(u, 0, h), halves)].rearrange("p (c i j) -> p c j i", i=REST_I, j=PACK),
+                out=parts[:, span(2 * i + 1, 1)].rearrange("p (c i j) -> p c j i", i=REST_RUN, j=PACK),
+                in0=w_sb[i][:].rearrange("p j (c i) -> p c j i", i=REST_RUN),
+                in1=parts[:, span(2 * i, 1)].rearrange("p (c i j) -> p c j i", i=REST_RUN, j=PACK),
                 op=ALU.subtract,
             )
 
-        def quantize(u, first, count):
+        def quantize(first, count):
             cols = slice(first * P, (first + count) * P)
             nc.vector.quantize_mx(
-                out=codes[u][:, cols].bitcast(FP8X4),
-                scales=scales[u][:, cols],
-                in_=hl[u][:, span(first, count)],
+                out=codes[:, cols].bitcast(FP8X4),
+                scales=scales[:, cols],
+                in_=parts[:, span(first, count)],
             )
 
         def gather_words(a):
@@ -132,100 +119,72 @@ def tile_list_tabw_hl_bias_kernel(tc, tab, w, b, offs, out):
         def gather_scales():
             nc.vector.tensor_copy(picked_scales[:], planes[:].bitcast(U8).indirect(offsets[:]))
 
-        banks = {}
-        for m in range(4):
-            ranges = [(0, 512)] if m < 3 else [(0, 256), (256, 256)]
-            banks[m] = [(j0, jn, psum.tile([P, 512], F32, name="acc%d_%d" % (m, j0))) for j0, jn in ranges]
-        done = {m: 0 for m in range(4)}
+        nc.scalar.dma_start(out=bias_rows[spare:P, :], in_=b.rearrange("(m p) -> m p", p=P))
 
-        def multiply(u, part, h):
-            a, m = units[u][h]
-            cols = slice(place(u, part, h) * P, (place(u, part, h) + 1) * P)
+        banks = []
+        for m in range(TILES):
+            ranges = [(0, S)] if m < TILES - 1 else [(0, S // 2), (S // 2, S // 2)]
+            banks.append([(j0, jn, psum.tile([P, S], F32, name="acc%d_%d" % (m, j0))) for j0, jn in ranges])
+
+        def finish(m):
+            for j0, jn, acc in banks[m]:
+                res = keep.tile([P, jn], F32, name="res%d_%d" % (m, j0), align_bytes=64)
+                if m == TILES - 1 and j0 == 0:
+                    nc.vector.tensor_scalar(res[:], acc[:, 0:jn], bias[:, m : m + 1], None, op0=ALU.add)
+                else:
+                    nc.scalar.activation(res[:], acc[:, 0:jn], ACT.Identity, bias=bias[:, m : m + 1])
+                nc.sync.dma_start(out=out[m * P : (m + 1) * P, j0 : j0 + jn], in_=res[:])
+
+        def multiply(g):
+            a, m = PIECES[g // 2]
+            is_lo = g % 2 == 1
+            closes = a == PASSES - 1 and is_lo
+            cols = slice(g * P, (g + 1) * P)
             for j0, jn, acc in banks[m]:
                 nc.tensor.matmul_mx(
                     out=acc[:, 0:jn],
-                    lhsT=codes[u][:, cols].bitcast(FP8X4),
-                    lhsT_scale=scales[u][:, cols],
+                    lhsT=codes[:, cols].bitcast(FP8X4),
+                    lhsT_scale=scales[:, cols],
                     rhs=picked[a][:, j0 : j0 + jn].bitcast(FP8X4),
-                    rhs_scale=picked_scales[4 * a : P, j0 : j0 + jn],
-                    start=(done[m] == 0),
-                    stop=(done[m] == 3),
+                    rhs_scale=picked_scales[SCALE_ROWS * a : P, j0 : j0 + jn],
+                    start=(a == 0 and not is_lo),
+                    stop=closes,
                 )
-            done[m] = done[m] + 1
+            if closes:
+                finish(m)
 
-        def finish(m, h, engine):
-            j0, jn, acc = banks[m][h]
-            res = keep.tile([P, jn], F32, name="res%d_%d" % (m, j0), align_bytes=64)
-            if engine == "scalar":
-                nc.scalar.activation(res[:], acc[:, 0:jn], ACT.Identity, bias=bias[:, m : m + 1])
-            else:
-                nc.vector.tensor_scalar(res[:], acc[:, 0:jn], bias[:, m : m + 1], None, op0=ALU.add)
-            nc.sync.dma_start(out=out[m * P : (m + 1) * P, j0 : j0 + jn], in_=res[:])
+        turned = psum.tile([P, P], F32, name="turned")
+        nc.tensor.transpose(turned[:], bias_rows[:], identity[:])
+        nc.scalar.copy(out=bias[:], in_=turned[:, spare:P])
 
-        load_bias()
-        turn_bias()
         load_table(0)
         nc.sync.dma_start(offsets[:], offs)
-        load_rows()
-        load_w(0, 0, 1)
-        load_w(0, 1, 1)
-        load_w(1, 0, 2)
-        load_table(1)
-        load_w(0, 2, 1)
-        load_w(1, 2, 1)
-        load_w(0, 3, 1)
-        load_w(1, 3, 1)
-        take_top(0, 0, 1)
-        take_top(0, 1, 1)
-        take_top(1, 0, 1)
-        take_top(1, 1, 1)
-        take_top(2, 0, 1)
-        take_top(2, 1, 1)
-        take_top(3, 0, 1)
-        take_top(3, 1, 1)
+        load_scale_rows()
+        for i in range(len(PIECES)):
+            if i == LOADED_BEFORE_TABLE_1:
+                load_table(1)
+            load_w(i)
+        for i in range(len(PIECES)):
+            take_top(i)
+
         gather_words(0)
         gather_scales()
-        mask(0, 0, 1)
-        rest(0, 0, 1)
-        mask(0, 1, 1)
-        quantize(0, 0, 2)
-        multiply(0, 0, 0)
-        multiply(0, 1, 0)
-        rest(0, 1, 1)
-        mask(1, 0, 1)
-        quantize(0, 2, 2)
-        multiply(0, 0, 1)
-        multiply(0, 1, 1)
-        mask(1, 1, 1)
-        gather_words(1)
-        quantize(1, 0, 2)
-        multiply(1, 0, 0)
-        multiply(1, 0, 1)
-        rest(1, 0, 2)
-        mask(2, 0, 2)
-        quantize(1, 2, 2)
-        multiply(1, 1, 0)
-        finish(0, 0, "scalar")
-        multiply(1, 1, 1)
-        finish(1, 0, "scalar")
-        rest(2, 0, 1)
-        quantize(2, 0, 2)
-        multiply(2, 0, 0)
-        multiply(2, 0, 1)
-        rest(2, 1, 1)
-        mask(3, 0, 2)
-        quantize(2, 2, 2)
-        multiply(2, 1, 0)
-        multiply(2, 1, 1)
-        finish(2, 0, "scalar")
-        rest(3, 0, 1)
-        quantize(3, 0, 2)
-        multiply(3, 0, 0)
-        multiply(3, 0, 1)
-        rest(3, 1, 1)
-        quantize(3, 2, 1)
-        multiply(3, 1, 0)
-        quantize(3, 3, 1)
-        multiply(3, 1, 1)
-        finish(3, 0, "vector")
-        finish(3, 1, "scalar")
+        mask(0)
+        last = len(PIECES) - 1
+        for i in range(last):
+            rest(i)
+            mask(i + 1)
+            if i == 0:
+                quantize(0, 1)
+            else:
+                quantize(2 * i - 1, 2)
+                multiply(2 * i - 1)
+            if i == FIRST_OF_PASS_1:
+                gather_words(1)
+            multiply(2 * i)
+        quantize(2 * last - 1, 1)
+        multiply(2 * last - 1)
+        rest(last)
+        for g in (2 * last, 2 * last + 1):
+            quantize(g, 1)
+            multiply(g)

@@ -22,7 +22,7 @@ TILES = M // P
 QUADRANT = 32
 SCALE_ROWS = 4
 HI_MASK = -983056
-TOP_RUN = 4
+TOP_RUN = 2
 REST_RUN = 2
 PIECES = [(0, 0), (0, 1), (1, 0), (1, 1), (0, 2), (1, 2), (0, 3), (1, 3)]
 FIRST_OF_PASS_1 = 2
@@ -75,9 +75,10 @@ def tile_list_tabw_hl_bias_kernel(tc, tab, w, b, offs, out):
 
         bias_rows = keep.tile([P, P], F32, name="bias_rows", align_bytes=64)
         identity = keep.tile([P, P], F32, name="identity", align_bytes=64)
+        spare = P - TILES
+        nc.scalar.dma_start(out=bias_rows[spare:P, :], in_=b.rearrange("(m p) -> m p", p=P))
         zero = keep.tile([P, 1], F32, name="zero")
         nc.vector.memset(zero[:], 0.0)
-        spare = P - TILES
         nc.scalar.activation(bias_rows[0:spare, :], zero[0:spare, :].to_broadcast([spare, P]), ACT.Identity)
         make_identity(nc, identity[:])
 
@@ -118,8 +119,6 @@ def tile_list_tabw_hl_bias_kernel(tc, tab, w, b, offs, out):
 
         def gather_scales():
             nc.vector.tensor_copy(picked_scales[:], planes[:].bitcast(U8).indirect(offsets[:]))
-
-        nc.scalar.dma_start(out=bias_rows[spare:P, :], in_=b.rearrange("(m p) -> m p", p=P))
 
         banks = []
         for m in range(TILES):

@@ -1,5 +1,4 @@
 import concourse.mybir as mybir
-from concourse.masks import make_identity
 
 K, M, T, S = 1024, 512, 1024, 512
 FLOPS = 2 * 2 * K * M * S
@@ -38,7 +37,7 @@ def tile_list_tabw_hl_bias_kernel(tc, tab, w, b, offs, out):
         offsets = keep.tile([P, S // 16], U16, name="offsets")
         planes = keep.tile([P, T // 4], I32, name="planes", align_bytes=64)
         bias = keep.tile([P, TILES], F32, name="bias")
-        nc.gpsimd.memset(planes[:], 0)
+        nc.vector.memset(planes[:], 0)
 
         groups = 2 * len(PIECES)
         top = keep.tile([P, len(PIECES) * P * PACK], BF16, name="top", align_bytes=64)
@@ -80,7 +79,18 @@ def tile_list_tabw_hl_bias_kernel(tc, tab, w, b, offs, out):
         zero = keep.tile([P, 1], F32, name="zero")
         nc.vector.memset(zero[:], 0.0)
         nc.scalar.activation(bias_rows[0:spare, :], zero[0:spare, :].to_broadcast([spare, P]), ACT.Identity)
-        make_identity(nc, identity[:])
+        ones = keep.tile([P, P], F32, name="ones", align_bytes=64)
+        column = keep.tile([P, P], F32, name="column", align_bytes=64)
+        corner = keep.tile([P, 1], F32, name="corner")
+        shifted = keep.tile([P, QUADRANT], F32, name="shifted", align_bytes=64)
+        row = keep.tile([P, QUADRANT], F32, name="row", align_bytes=64)
+        nc.vector.memset(ones[:], 1.0)
+        for q in range(P // QUADRANT):
+            nc.vector.memset(corner[QUADRANT * q : QUADRANT * (q + 1), :], float(QUADRANT * q))
+        nc.vector.tensor_tensor_scan(column[:], ones[:], ones[:], 0.0, ALU.mult, ALU.add)
+        nc.vector.tensor_scalar(shifted[:], column[:, 0:QUADRANT], corner[:], None, op0=ALU.add)
+        nc.vector.transpose(row[:], shifted[:])
+        nc.vector.tensor_scalar(identity[:], column[:], row[:, 0:1], None, op0=ALU.is_equal)
 
         def span(first, count):
             return slice(first * P * PACK, (first + count) * P * PACK)

@@ -21,6 +21,7 @@ TILES = M // P
 QUADRANT = 32
 SCALE_ROWS = 4
 HI_MASK = -983056
+HI_MASK_F32 = -1048576
 TOP_RUN = 2
 REST_RUN = 2
 PIECES = [(0, 0), (0, 1), (1, 0), (1, 1), (0, 2), (1, 2), (0, 3), (1, 3)]
@@ -76,7 +77,7 @@ def tile_list_tabw_hl_bias_kernel(tc, tab, w, b, offs, out):
         identity = keep.tile([P, P], F32, name="identity", align_bytes=64)
         spare = P - TILES
         nc.scalar.dma_start(out=bias_rows[spare:P, :], in_=b.rearrange("(m p) -> m p", p=P))
-        zero = keep.tile([P, 1], F32, name="zero")
+        zero = keep.tile([P, 1], F32, name="zero", tag="zero", align_bytes=64)
         nc.vector.memset(zero[:], 0.0)
         nc.scalar.activation(bias_rows[0:spare, :], zero[0:spare, :].to_broadcast([spare, P]), ACT.Identity)
         ones = keep.tile([P, P], F32, name="ones", align_bytes=64)
@@ -97,7 +98,11 @@ def tile_list_tabw_hl_bias_kernel(tc, tab, w, b, offs, out):
 
         def take_top(i):
             upper = w_sb[i][:].bitcast(BF16).rearrange("p j (c i e) -> p c j i e", i=TOP_RUN, e=2)[:, :, :, :, 1]
-            nc.scalar.copy(out=top[:, span(i, 1)].rearrange("p (c i j) -> p c j i", i=TOP_RUN, j=PACK), in_=upper)
+            woven = top[:, span(i, 1)].rearrange("p (c i j) -> p c j i", i=TOP_RUN, j=PACK)
+            if i == 1:
+                nc.scalar.activation(woven, upper, ACT.Identity, bias=zero[:])
+            else:
+                nc.scalar.copy(out=woven, in_=upper)
 
         def mask(i):
             nc.vector.tensor_scalar(
@@ -115,6 +120,25 @@ def tile_list_tabw_hl_bias_kernel(tc, tab, w, b, offs, out):
                 in1=parts[:, span(2 * i, 1)].rearrange("p (c i j) -> p c j i", i=REST_RUN, j=PACK),
                 op=ALU.subtract,
             )
+
+        hi_first = keep.tile([P, PACK, P], F32, name="hi_first", align_bytes=64)
+
+        def cut_first():
+            nc.vector.tensor_scalar(
+                hi_first[:].bitcast(I32), w_sb[0][:].bitcast(I32), HI_MASK_F32, None, op0=ALU.bitwise_and
+            )
+
+        def rest_first():
+            nc.vector.tensor_tensor(
+                out=parts[:, span(1, 1)].rearrange("p (c i j) -> p c j i", i=REST_RUN, j=PACK),
+                in0=w_sb[0][:].rearrange("p j (c i) -> p c j i", i=REST_RUN),
+                in1=hi_first[:].rearrange("p j (c i) -> p c j i", i=REST_RUN),
+                op=ALU.subtract,
+            )
+
+        def weave_first():
+            upper = hi_first[:].bitcast(BF16).rearrange("p j (c i e) -> p c j i e", i=TOP_RUN, e=2)[:, :, :, :, 1]
+            nc.scalar.copy(out=parts[:, span(0, 1)].rearrange("p (c i j) -> p c j i", i=TOP_RUN, j=PACK), in_=upper)
 
         def quantize(first, count):
             cols = slice(first * P, (first + count) * P)
@@ -144,7 +168,7 @@ def tile_list_tabw_hl_bias_kernel(tc, tab, w, b, offs, out):
                     nc.scalar.activation(res[:], acc[:, 0:jn], ACT.Identity, bias=bias[:, m : m + 1])
                 nc.sync.dma_start(out=out[m * P : (m + 1) * P, j0 : j0 + jn], in_=res[:])
 
-        def multiply(g):
+        def multiply(g, own_codes=None):
             a, m = PIECES[g // 2]
             is_lo = g % 2 == 1
             closes = a == PASSES - 1 and is_lo
@@ -152,7 +176,7 @@ def tile_list_tabw_hl_bias_kernel(tc, tab, w, b, offs, out):
             for j0, jn, acc in banks[m]:
                 nc.tensor.matmul_mx(
                     out=acc[:, 0:jn],
-                    lhsT=codes[:, cols].bitcast(FP8X4),
+                    lhsT=(codes[:, cols] if own_codes is None else own_codes).bitcast(FP8X4),
                     lhsT_scale=scales[:, cols],
                     rhs=picked[a][:, j0 : j0 + jn].bitcast(FP8X4),
                     rhs_scale=picked_scales[SCALE_ROWS * a : P, j0 : j0 + jn],
@@ -166,25 +190,36 @@ def tile_list_tabw_hl_bias_kernel(tc, tab, w, b, offs, out):
         nc.tensor.transpose(turned[:], bias_rows[:], identity[:])
         nc.scalar.copy(out=bias[:], in_=turned[:, spare:P])
 
-        load_table(0)
+        load_w(0)
         nc.sync.dma_start(offsets[:], offs)
+        load_table(0)
         load_scale_rows()
-        for i in range(len(PIECES)):
+        for i in range(1, len(PIECES)):
             if i == LOADED_BEFORE_TABLE_1:
                 load_table(1)
             load_w(i)
-        for i in range(len(PIECES)):
+        cut_first()
+        rest_first()
+        weave_first()
+        for i in range(1, len(PIECES)):
             take_top(i)
 
+        quantize(0, 1)
         gather_words(0)
         gather_scales()
-        mask(0)
+        multiply(0)
+        mask(1)
+        first_codes = keep.tile([P, P], U32, name="first_codes", tag="zero", align_bytes=64)
+        nc.vector.quantize_mx(
+            out=first_codes[:].bitcast(FP8X4), scales=scales[:, P : 2 * P], in_=parts[:, span(1, 1)]
+        )
+        multiply(1, first_codes[:])
         last = len(PIECES) - 1
-        for i in range(last):
+        for i in range(1, last):
             rest(i)
             mask(i + 1)
-            if i == 0:
-                quantize(0, 1)
+            if i == 1:
+                quantize(2, 1)
             else:
                 quantize(2 * i - 1, 2)
                 multiply(2 * i - 1)

@@ -83,15 +83,13 @@ def tile_list_tabw_hl_bias_kernel(tc, tab, w, b, offs, out):
         ones = keep.tile([P, P], F32, name="ones", align_bytes=64)
         column = keep.tile([P, P], F32, name="column", align_bytes=64)
         corner = keep.tile([P, 1], F32, name="corner")
-        shifted = keep.tile([P, QUADRANT], F32, name="shifted", align_bytes=64)
         row = keep.tile([P, QUADRANT], F32, name="row", align_bytes=64)
         nc.vector.memset(ones[:], 1.0)
         for q in range(P // QUADRANT):
             nc.vector.memset(corner[QUADRANT * q : QUADRANT * (q + 1), :], float(QUADRANT * q))
         nc.vector.tensor_tensor_scan(column[:], ones[:], ones[:], 0.0, ALU.mult, ALU.add)
-        nc.vector.tensor_scalar(shifted[:], column[:, 0:QUADRANT], corner[:], None, op0=ALU.add)
-        nc.vector.transpose(row[:], shifted[:])
-        nc.vector.tensor_scalar(identity[:], column[:], row[:, 0:1], None, op0=ALU.is_equal)
+        nc.vector.transpose(row[:], column[:, 0:QUADRANT])
+        nc.vector.tensor_scalar(identity[:], column[:], corner[:], row[:, 0:1], op0=ALU.subtract, op1=ALU.is_equal)
 
         def span(first, count):
             return slice(first * P * PACK, (first + count) * P * PACK)
@@ -204,28 +202,30 @@ def tile_list_tabw_hl_bias_kernel(tc, tab, w, b, offs, out):
         for i in range(1, len(PIECES)):
             take_top(i)
 
-        quantize(0, 1)
         gather_words(0)
         gather_scales()
-        multiply(0)
         mask(1)
-        first_codes = keep.tile([P, P], U32, name="first_codes", tag="zero", align_bytes=64)
+        first_codes = keep.tile([P, 2 * P], U32, name="first_codes", tag="zero", align_bytes=64)
         nc.vector.quantize_mx(
-            out=first_codes[:].bitcast(FP8X4), scales=scales[:, P : 2 * P], in_=parts[:, span(1, 1)]
+            out=first_codes[:].bitcast(FP8X4), scales=scales[:, 0 : 2 * P], in_=parts[:, span(0, 2)]
         )
-        multiply(1, first_codes[:])
+        multiply(0, first_codes[:, 0:P])
+        multiply(1, first_codes[:, P : 2 * P])
         last = len(PIECES) - 1
         for i in range(1, last):
             rest(i)
             mask(i + 1)
-            if i == 1:
-                quantize(2, 1)
+            if i <= FIRST_OF_PASS_1:
+                quantize(2 * i, 1)
             else:
                 quantize(2 * i - 1, 2)
                 multiply(2 * i - 1)
             if i == FIRST_OF_PASS_1:
                 gather_words(1)
             multiply(2 * i)
+            if i < FIRST_OF_PASS_1:
+                quantize(2 * i + 1, 1)
+                multiply(2 * i + 1)
         quantize(2 * last - 1, 1)
         multiply(2 * last - 1)
         rest(last)

@@ -24,9 +24,9 @@ HI_MASK = -983056
 HI_MASK_F32 = -1048576
 TOP_RUN = 2
 REST_RUN = 2
-PIECES = [(0, 0), (0, 1), (1, 0), (1, 1), (0, 2), (1, 2), (0, 3), (1, 3)]
-FIRST_OF_PASS_1 = 2
-LOADED_BEFORE_TABLE_1 = 4
+PIECES = [(0, 0), (0, 1), (0, 2), (1, 0), (1, 1), (1, 2), (0, 3), (1, 3)]
+FIRST_OF_PASS_1 = 3
+LOADED_BEFORE_TABLE_1 = 5
 
 
 def tile_list_tabw_hl_bias_kernel(tc, tab, w, b, offs, out):

@@ -26,6 +26,7 @@ TOP_RUN = 2
 REST_RUN = 2
 PIECES = [(0, 0), (0, 1), (0, 2), (1, 0), (1, 1), (1, 2), (0, 3), (1, 3)]
 FIRST_OF_PASS_1 = 3
+LOADED_BEFORE_TABLE_0 = 2
 LOADED_BEFORE_TABLE_1 = 5
 
 
@@ -76,9 +77,10 @@ def tile_list_tabw_hl_bias_kernel(tc, tab, w, b, offs, out):
         bias_rows = keep.tile([P, P], F32, name="bias_rows", align_bytes=64)
         identity = keep.tile([P, P], F32, name="identity", align_bytes=64)
         spare = P - TILES
-        nc.scalar.dma_start(out=bias_rows[spare:P, :], in_=b.rearrange("(m p) -> m p", p=P))
         zero = keep.tile([P, 1], F32, name="zero", tag="zero", align_bytes=64)
+        zero_next = keep.tile([P, 1], F32, name="zero_next", tag="zero_next", align_bytes=64)
         nc.vector.memset(zero[:], 0.0)
+        nc.vector.memset(zero_next[:], 0.0)
         nc.scalar.activation(bias_rows[0:spare, :], zero[0:spare, :].to_broadcast([spare, P]), ACT.Identity)
         ones = keep.tile([P, P], F32, name="ones", align_bytes=64)
         column = keep.tile([P, P], F32, name="column", align_bytes=64)
@@ -97,8 +99,8 @@ def tile_list_tabw_hl_bias_kernel(tc, tab, w, b, offs, out):
         def take_top(i):
             upper = w_sb[i][:].bitcast(BF16).rearrange("p j (c i e) -> p c j i e", i=TOP_RUN, e=2)[:, :, :, :, 1]
             woven = top[:, span(i, 1)].rearrange("p (c i j) -> p c j i", i=TOP_RUN, j=PACK)
-            if i == 1:
-                nc.scalar.activation(woven, upper, ACT.Identity, bias=zero[:])
+            if i <= 2:
+                nc.scalar.activation(woven, upper, ACT.Identity, bias=(zero if i == 1 else zero_next)[:])
             else:
                 nc.scalar.copy(out=woven, in_=upper)
 
@@ -121,18 +123,27 @@ def tile_list_tabw_hl_bias_kernel(tc, tab, w, b, offs, out):
 
         hi_first = keep.tile([P, PACK, P], F32, name="hi_first", align_bytes=64)
 
+        halves = [slice(0, P // 2), slice(P // 2, P)]
+
         def cut_first():
-            nc.vector.tensor_scalar(
-                hi_first[:].bitcast(I32), w_sb[0][:].bitcast(I32), HI_MASK_F32, None, op0=ALU.bitwise_and
-            )
+            for cols in halves:
+                nc.vector.tensor_scalar(
+                    hi_first[:, :, cols].bitcast(I32),
+                    w_sb[0][:, :, cols].bitcast(I32),
+                    HI_MASK_F32,
+                    None,
+                    op0=ALU.bitwise_and,
+                )
 
         def rest_first():
-            nc.vector.tensor_tensor(
-                out=parts[:, span(1, 1)].rearrange("p (c i j) -> p c j i", i=REST_RUN, j=PACK),
-                in0=w_sb[0][:].rearrange("p j (c i) -> p c j i", i=REST_RUN),
-                in1=hi_first[:].rearrange("p j (c i) -> p c j i", i=REST_RUN),
-                op=ALU.subtract,
-            )
+            lo = parts[:, span(1, 1)]
+            for cols in halves:
+                nc.vector.tensor_tensor(
+                    out=lo[:, PACK * cols.start : PACK * cols.stop].rearrange("p (c i j) -> p c j i", i=REST_RUN, j=PACK),
+                    in0=w_sb[0][:, :, cols].rearrange("p j (c i) -> p c j i", i=REST_RUN),
+                    in1=hi_first[:, :, cols].rearrange("p j (c i) -> p c j i", i=REST_RUN),
+                    op=ALU.subtract,
+                )
 
         def weave_first():
             upper = hi_first[:].bitcast(BF16).rearrange("p j (c i e) -> p c j i e", i=TOP_RUN, e=2)[:, :, :, :, 1]
@@ -184,35 +195,44 @@ def tile_list_tabw_hl_bias_kernel(tc, tab, w, b, offs, out):
             if closes:
                 finish(m)
 
-        turned = psum.tile([P, P], F32, name="turned")
-        nc.tensor.transpose(turned[:], bias_rows[:], identity[:])
-        nc.scalar.copy(out=bias[:], in_=turned[:, spare:P])
-
         load_w(0)
+        nc.sync.dma_start(out=bias_rows[spare:P, :], in_=b.rearrange("(m p) -> m p", p=P))
         nc.sync.dma_start(offsets[:], offs)
-        load_table(0)
         load_scale_rows()
         for i in range(1, len(PIECES)):
+            if i == LOADED_BEFORE_TABLE_0:
+                load_table(0)
             if i == LOADED_BEFORE_TABLE_1:
                 load_table(1)
             load_w(i)
+        turned = psum.tile([P, P], F32, name="turned")
+        nc.tensor.transpose(turned[:], bias_rows[:], identity[:])
+        nc.scalar.copy(out=bias[:], in_=turned[:, spare:P])
         cut_first()
         rest_first()
         weave_first()
         for i in range(1, len(PIECES)):
             take_top(i)
 
-        gather_words(0)
         gather_scales()
         mask(1)
         first_codes = keep.tile([P, 2 * P], U32, name="first_codes", tag="zero", align_bytes=64)
         nc.vector.quantize_mx(
             out=first_codes[:].bitcast(FP8X4), scales=scales[:, 0 : 2 * P], in_=parts[:, span(0, 2)]
         )
+        rest(1)
+        gather_words(0)
         multiply(0, first_codes[:, 0:P])
         multiply(1, first_codes[:, P : 2 * P])
+        mask(2)
+        next_codes = keep.tile([P, 2 * P], U32, name="next_codes", tag="zero_next", align_bytes=64)
+        nc.vector.quantize_mx(
+            out=next_codes[:].bitcast(FP8X4), scales=scales[:, 2 * P : 4 * P], in_=parts[:, span(2, 2)]
+        )
+        multiply(2, next_codes[:, 0:P])
+        multiply(3, next_codes[:, P : 2 * P])
         last = len(PIECES) - 1
-        for i in range(1, last):
+        for i in range(2, last):
             rest(i)
             mask(i + 1)
             if i <= FIRST_OF_PASS_1:

@@ -78,11 +78,9 @@ def tile_list_tabw_hl_bias_kernel(tc, tab, w, b, offs, out):
         identity = keep.tile([P, P], F32, name="identity", align_bytes=64)
         spare = P - TILES
         zero = keep.tile([P, 1], F32, name="zero", tag="zero", align_bytes=64)
-        zero_next = keep.tile([P, 1], F32, name="zero_next", tag="zero_next", align_bytes=64)
         nc.vector.memset(zero[:], 0.0)
-        nc.vector.memset(zero_next[:], 0.0)
         nc.scalar.activation(bias_rows[0:spare, :], zero[0:spare, :].to_broadcast([spare, P]), ACT.Identity)
-        ones = keep.tile([P, P], F32, name="ones", align_bytes=64)
+        ones = keep.tile([P, P], F32, name="ones", tag="ones", align_bytes=64)
         column = keep.tile([P, P], F32, name="column", align_bytes=64)
         corner = keep.tile([P, 1], F32, name="corner")
         row = keep.tile([P, QUADRANT], F32, name="row", align_bytes=64)
@@ -99,8 +97,10 @@ def tile_list_tabw_hl_bias_kernel(tc, tab, w, b, offs, out):
         def take_top(i):
             upper = w_sb[i][:].bitcast(BF16).rearrange("p j (c i e) -> p c j i e", i=TOP_RUN, e=2)[:, :, :, :, 1]
             woven = top[:, span(i, 1)].rearrange("p (c i j) -> p c j i", i=TOP_RUN, j=PACK)
-            if i <= 2:
-                nc.scalar.activation(woven, upper, ACT.Identity, bias=(zero if i == 1 else zero_next)[:])
+            if i == 1:
+                nc.scalar.activation(woven, upper, ACT.Identity, bias=zero[:])
+            elif i == 2:
+                nc.scalar.activation(woven, upper, ACT.Identity, scale=ones[:, 0:1])
             else:
                 nc.scalar.copy(out=woven, in_=upper)
 
@@ -195,9 +195,9 @@ def tile_list_tabw_hl_bias_kernel(tc, tab, w, b, offs, out):
             if closes:
                 finish(m)
 
+        nc.sync.dma_start(offsets[:], offs)
         load_w(0)
         nc.sync.dma_start(out=bias_rows[spare:P, :], in_=b.rearrange("(m p) -> m p", p=P))
-        nc.sync.dma_start(offsets[:], offs)
         load_scale_rows()
         for i in range(1, len(PIECES)):
             if i == LOADED_BEFORE_TABLE_0:
@@ -225,7 +225,7 @@ def tile_list_tabw_hl_bias_kernel(tc, tab, w, b, offs, out):
         multiply(0, first_codes[:, 0:P])
         multiply(1, first_codes[:, P : 2 * P])
         mask(2)
-        next_codes = keep.tile([P, 2 * P], U32, name="next_codes", tag="zero_next", align_bytes=64)
+        next_codes = keep.tile([P, 2 * P], U32, name="next_codes", tag="ones", align_bytes=64)
         nc.vector.quantize_mx(
             out=next_codes[:].bitcast(FP8X4), scales=scales[:, 2 * P : 4 * P], in_=parts[:, span(2, 2)]
         )

@@ -20,14 +20,12 @@ PASSES = K // K_PASS
 TILES = M // P
 QUADRANT = 32
 SCALE_ROWS = 4
-HI_MASK = -983056
+HI_MASK_PAIR = -983056
 HI_MASK_F32 = -1048576
-TOP_RUN = 2
-REST_RUN = 2
-PIECES = [(0, 0), (0, 1), (0, 2), (1, 0), (1, 1), (1, 2), (0, 3), (1, 3)]
-FIRST_OF_PASS_1 = 3
-LOADED_BEFORE_TABLE_0 = 2
-LOADED_BEFORE_TABLE_1 = 5
+RUN = 2
+PIECES = [(a, m) for a in range(PASSES) for m in range(TILES - 1)] + [(a, TILES - 1) for a in range(PASSES)]
+SCALES_AFTER = 0
+WORDS_AFTER = (2, 4)
 
 
 def tile_list_tabw_hl_bias_kernel(tc, tab, w, b, offs, out):
@@ -42,6 +40,7 @@ def tile_list_tabw_hl_bias_kernel(tc, tab, w, b, offs, out):
         nc.vector.memset(planes[:], 0)
 
         groups = 2 * len(PIECES)
+        last = len(PIECES) - 1
         top = keep.tile([P, len(PIECES) * P * PACK], BF16, name="top", align_bytes=64)
         parts = keep.tile([P, groups * P * PACK], BF16, name="parts", align_bytes=64)
         codes = keep.tile([P, groups * P], U32, name="codes", align_bytes=64)
@@ -81,7 +80,7 @@ def tile_list_tabw_hl_bias_kernel(tc, tab, w, b, offs, out):
         nc.vector.memset(zero[:], 0.0)
         nc.scalar.activation(bias_rows[0:spare, :], zero[0:spare, :].to_broadcast([spare, P]), ACT.Identity)
         ones = keep.tile([P, P], F32, name="ones", tag="ones", align_bytes=64)
-        column = keep.tile([P, P], F32, name="column", align_bytes=64)
+        column = keep.tile([P, P], F32, name="column", tag="column", align_bytes=64)
         corner = keep.tile([P, 1], F32, name="corner")
         row = keep.tile([P, QUADRANT], F32, name="row", align_bytes=64)
         nc.vector.memset(ones[:], 1.0)
@@ -91,41 +90,50 @@ def tile_list_tabw_hl_bias_kernel(tc, tab, w, b, offs, out):
         nc.vector.transpose(row[:], column[:, 0:QUADRANT])
         nc.vector.tensor_scalar(identity[:], column[:], corner[:], row[:, 0:1], op0=ALU.subtract, op1=ALU.is_equal)
 
+        shared = {
+            SCALES_AFTER: ("zero", {"bias": zero[:]}),
+            WORDS_AFTER[0]: ("ones", {"scale": ones[:, 0:1]}),
+            WORDS_AFTER[1]: ("column", {"scale": column[:, 0:1]}),
+        }
+
         def span(first, count):
             return slice(first * P * PACK, (first + count) * P * PACK)
 
+        def woven(view):
+            return view.rearrange("p (c i j) -> p c j i", i=RUN, j=PACK)
+
+        def rows(view):
+            return view.rearrange("p j (c i) -> p c j i", i=RUN)
+
+        def upper_halves(piece):
+            return piece[:].bitcast(BF16).rearrange("p j (c i e) -> p c j i e", i=RUN, e=2)[:, :, :, :, 1]
+
         def take_top(i):
-            upper = w_sb[i][:].bitcast(BF16).rearrange("p j (c i e) -> p c j i e", i=TOP_RUN, e=2)[:, :, :, :, 1]
-            woven = top[:, span(i, 1)].rearrange("p (c i j) -> p c j i", i=TOP_RUN, j=PACK)
-            if i == 1:
-                nc.scalar.activation(woven, upper, ACT.Identity, bias=zero[:])
-            elif i == 2:
-                nc.scalar.activation(woven, upper, ACT.Identity, scale=ones[:, 0:1])
+            if i - 1 in shared:
+                nc.scalar.activation(woven(top[:, span(i, 1)]), upper_halves(w_sb[i]), ACT.Identity, **shared[i - 1][1])
             else:
-                nc.scalar.copy(out=woven, in_=upper)
+                nc.scalar.copy(out=woven(top[:, span(i, 1)]), in_=upper_halves(w_sb[i]))
 
         def mask(i):
             nc.vector.tensor_scalar(
                 parts[:, span(2 * i, 1)].bitcast(I32),
                 top[:, span(i, 1)].bitcast(I32),
-                HI_MASK,
+                HI_MASK_PAIR,
                 None,
                 op0=ALU.bitwise_and,
             )
 
         def rest(i):
             nc.vector.tensor_tensor(
-                out=parts[:, span(2 * i + 1, 1)].rearrange("p (c i j) -> p c j i", i=REST_RUN, j=PACK),
-                in0=w_sb[i][:].rearrange("p j (c i) -> p c j i", i=REST_RUN),
-                in1=parts[:, span(2 * i, 1)].rearrange("p (c i j) -> p c j i", i=REST_RUN, j=PACK),
+                out=woven(parts[:, span(2 * i + 1, 1)]),
+                in0=rows(w_sb[i][:]),
+                in1=woven(parts[:, span(2 * i, 1)]),
                 op=ALU.subtract,
             )
 
-        hi_first = keep.tile([P, PACK, P], F32, name="hi_first", align_bytes=64)
-
-        halves = [slice(0, P // 2), slice(P // 2, P)]
-
-        def cut_first():
+        def split_first():
+            hi_first = keep.tile([P, PACK, P], F32, name="hi_first", align_bytes=64)
+            halves = [slice(0, P // 2), slice(P // 2, P)]
             for cols in halves:
                 nc.vector.tensor_scalar(
                     hi_first[:, :, cols].bitcast(I32),
@@ -134,28 +142,34 @@ def tile_list_tabw_hl_bias_kernel(tc, tab, w, b, offs, out):
                     None,
                     op0=ALU.bitwise_and,
                 )
-
-        def rest_first():
-            lo = parts[:, span(1, 1)]
+            lo_first = parts[:, span(1, 1)]
             for cols in halves:
                 nc.vector.tensor_tensor(
-                    out=lo[:, PACK * cols.start : PACK * cols.stop].rearrange("p (c i j) -> p c j i", i=REST_RUN, j=PACK),
-                    in0=w_sb[0][:, :, cols].rearrange("p j (c i) -> p c j i", i=REST_RUN),
-                    in1=hi_first[:, :, cols].rearrange("p j (c i) -> p c j i", i=REST_RUN),
+                    out=woven(lo_first[:, PACK * cols.start : PACK * cols.stop]),
+                    in0=rows(w_sb[0][:, :, cols]),
+                    in1=rows(hi_first[:, :, cols]),
                     op=ALU.subtract,
                 )
+            nc.scalar.copy(out=woven(parts[:, span(0, 1)]), in_=upper_halves(hi_first))
 
-        def weave_first():
-            upper = hi_first[:].bitcast(BF16).rearrange("p j (c i e) -> p c j i e", i=TOP_RUN, e=2)[:, :, :, :, 1]
-            nc.scalar.copy(out=parts[:, span(0, 1)].rearrange("p (c i j) -> p c j i", i=TOP_RUN, j=PACK), in_=upper)
+        group_codes = [codes[:, g * P : (g + 1) * P] for g in range(groups)]
 
-        def quantize(first, count):
-            cols = slice(first * P, (first + count) * P)
+        def quantize(target, first, count):
             nc.vector.quantize_mx(
-                out=codes[:, cols].bitcast(FP8X4),
-                scales=scales[:, cols],
+                out=target.bitcast(FP8X4),
+                scales=scales[:, first * P : (first + count) * P],
                 in_=parts[:, span(first, count)],
             )
+
+        def quantize_piece(i):
+            if i in shared:
+                pair = keep.tile([P, 2 * P], U32, name="pair%d" % i, tag=shared[i][0], align_bytes=64)
+                group_codes[2 * i] = pair[:, 0:P]
+                group_codes[2 * i + 1] = pair[:, P : 2 * P]
+                quantize(pair[:], 2 * i, 2)
+            else:
+                for g in (2 * i, 2 * i + 1):
+                    quantize(group_codes[g], g, 1)
 
         def gather_words(a):
             nc.vector.tensor_copy(picked[a][:], words[a][:].bitcast(U32).indirect(offsets[:]))
@@ -177,22 +191,25 @@ def tile_list_tabw_hl_bias_kernel(tc, tab, w, b, offs, out):
                     nc.scalar.activation(res[:], acc[:, 0:jn], ACT.Identity, bias=bias[:, m : m + 1])
                 nc.sync.dma_start(out=out[m * P : (m + 1) * P, j0 : j0 + jn], in_=res[:])
 
-        def multiply(g, own_codes=None):
-            a, m = PIECES[g // 2]
-            is_lo = g % 2 == 1
-            closes = a == PASSES - 1 and is_lo
-            cols = slice(g * P, (g + 1) * P)
-            for j0, jn, acc in banks[m]:
-                nc.tensor.matmul_mx(
-                    out=acc[:, 0:jn],
-                    lhsT=(codes[:, cols] if own_codes is None else own_codes).bitcast(FP8X4),
-                    lhsT_scale=scales[:, cols],
-                    rhs=picked[a][:, j0 : j0 + jn].bitcast(FP8X4),
-                    rhs_scale=picked_scales[SCALE_ROWS * a : P, j0 : j0 + jn],
-                    start=(a == 0 and not is_lo),
-                    stop=closes,
-                )
-            if closes:
+        def one_pass(g, bank, opens, closes):
+            a = PIECES[g // 2][0]
+            j0, jn, acc = bank
+            nc.tensor.matmul_mx(
+                out=acc[:, 0:jn],
+                lhsT=group_codes[g].bitcast(FP8X4),
+                lhsT_scale=scales[:, g * P : (g + 1) * P],
+                rhs=picked[a][:, j0 : j0 + jn].bitcast(FP8X4),
+                rhs_scale=picked_scales[SCALE_ROWS * a : P, j0 : j0 + jn],
+                start=opens,
+                stop=closes,
+            )
+
+        def multiply(i):
+            a, m = PIECES[i]
+            for is_lo in (False, True):
+                for bank in banks[m]:
+                    one_pass(2 * i + is_lo, bank, a == 0 and not is_lo, a == PASSES - 1 and is_lo)
+            if a == PASSES - 1:
                 finish(m)
 
         nc.sync.dma_start(offsets[:], offs)
@@ -200,55 +217,39 @@ def tile_list_tabw_hl_bias_kernel(tc, tab, w, b, offs, out):
         nc.sync.dma_start(out=bias_rows[spare:P, :], in_=b.rearrange("(m p) -> m p", p=P))
         load_scale_rows()
         for i in range(1, len(PIECES)):
-            if i == LOADED_BEFORE_TABLE_0:
-                load_table(0)
-            if i == LOADED_BEFORE_TABLE_1:
-                load_table(1)
             load_w(i)
+            if i in WORDS_AFTER:
+                load_table(WORDS_AFTER.index(i))
         turned = psum.tile([P, P], F32, name="turned")
         nc.tensor.transpose(turned[:], bias_rows[:], identity[:])
         nc.scalar.copy(out=bias[:], in_=turned[:, spare:P])
-        cut_first()
-        rest_first()
-        weave_first()
+        split_first()
         for i in range(1, len(PIECES)):
             take_top(i)
 
-        gather_scales()
-        mask(1)
-        first_codes = keep.tile([P, 2 * P], U32, name="first_codes", tag="zero", align_bytes=64)
-        nc.vector.quantize_mx(
-            out=first_codes[:].bitcast(FP8X4), scales=scales[:, 0 : 2 * P], in_=parts[:, span(0, 2)]
-        )
-        rest(1)
-        gather_words(0)
-        multiply(0, first_codes[:, 0:P])
-        multiply(1, first_codes[:, P : 2 * P])
-        mask(2)
-        next_codes = keep.tile([P, 2 * P], U32, name="next_codes", tag="ones", align_bytes=64)
-        nc.vector.quantize_mx(
-            out=next_codes[:].bitcast(FP8X4), scales=scales[:, 2 * P : 4 * P], in_=parts[:, span(2, 2)]
-        )
-        multiply(2, next_codes[:, 0:P])
-        multiply(3, next_codes[:, P : 2 * P])
-        last = len(PIECES) - 1
-        for i in range(2, last):
-            rest(i)
+        waiting = []
+        for i in range(last):
+            if i > 0:
+                rest(i)
+            if i == SCALES_AFTER:
+                gather_scales()
+            if i in WORDS_AFTER:
+                gather_words(WORDS_AFTER.index(i))
+                for earlier in waiting:
+                    multiply(earlier)
+                waiting.clear()
             mask(i + 1)
-            if i <= FIRST_OF_PASS_1:
-                quantize(2 * i, 1)
+            quantize_piece(i)
+            if i < WORDS_AFTER[PIECES[i][0]]:
+                waiting.append(i)
             else:
-                quantize(2 * i - 1, 2)
-                multiply(2 * i - 1)
-            if i == FIRST_OF_PASS_1:
-                gather_words(1)
-            multiply(2 * i)
-            if i < FIRST_OF_PASS_1:
-                quantize(2 * i + 1, 1)
-                multiply(2 * i + 1)
-        quantize(2 * last - 1, 1)
-        multiply(2 * last - 1)
+                multiply(i)
         rest(last)
-        for g in (2 * last, 2 * last + 1):
-            quantize(g, 1)
-            multiply(g)
+        quantize_piece(last)
+        hi, lo = 2 * last, 2 * last + 1
+        first_bank, second_bank = banks[TILES - 1]
+        one_pass(hi, first_bank, False, False)
+        one_pass(lo, first_bank, False, True)
+        one_pass(lo, second_bank, False, False)
+        one_pass(hi, second_bank, False, True)
+        finish(TILES - 1)

@@ -37,7 +37,8 @@ def tile_list_tabw_hl_bias_kernel(tc, tab, w, b, offs, out):
         offsets = keep.tile([P, S // 16], U16, name="offsets")
         planes = keep.tile([P, T // 4], I32, name="planes", align_bytes=64)
         bias = keep.tile([P, TILES], F32, name="bias")
-        nc.vector.memset(planes[:], 0)
+        nc.vector.memset(planes[:, 0 : T // 8], 0)
+        nc.gpsimd.memset(planes[:, T // 8 : T // 4], 0)
 
         groups = 2 * len(PIECES)
         last = len(PIECES) - 1
@@ -106,34 +107,40 @@ def tile_list_tabw_hl_bias_kernel(tc, tab, w, b, offs, out):
             return view.rearrange("p j (c i) -> p c j i", i=RUN)
 
         def upper_halves(piece):
-            return piece[:].bitcast(BF16).rearrange("p j (c i e) -> p c j i e", i=RUN, e=2)[:, :, :, :, 1]
+            return piece.bitcast(BF16).rearrange("p j (c i e) -> p c j i e", i=RUN, e=2)[:, :, :, :, 1]
 
-        def take_top(i):
-            if i - 1 in shared:
-                nc.scalar.activation(woven(top[:, span(i, 1)]), upper_halves(w_sb[i]), ACT.Identity, **shared[i - 1][1])
+        whole = slice(0, P)
+        halves = [slice(0, P // 2), slice(P // 2, P)]
+
+        def columns(tile, group, cols):
+            return tile[:, (group * P + cols.start) * PACK : (group * P + cols.stop) * PACK]
+
+        def take_top(i, cols=whole):
+            source = upper_halves(w_sb[i][:, :, cols])
+            if i - 1 in shared and cols.start == 0:
+                nc.scalar.activation(woven(columns(top, i, cols)), source, ACT.Identity, **shared[i - 1][1])
             else:
-                nc.scalar.copy(out=woven(top[:, span(i, 1)]), in_=upper_halves(w_sb[i]))
+                nc.scalar.copy(out=woven(columns(top, i, cols)), in_=source)
 
-        def mask(i):
+        def mask(i, cols=whole):
             nc.vector.tensor_scalar(
-                parts[:, span(2 * i, 1)].bitcast(I32),
-                top[:, span(i, 1)].bitcast(I32),
+                columns(parts, 2 * i, cols).bitcast(I32),
+                columns(top, i, cols).bitcast(I32),
                 HI_MASK_PAIR,
                 None,
                 op0=ALU.bitwise_and,
             )
 
-        def rest(i):
+        def rest(i, cols=whole):
             nc.vector.tensor_tensor(
-                out=woven(parts[:, span(2 * i + 1, 1)]),
-                in0=rows(w_sb[i][:]),
-                in1=woven(parts[:, span(2 * i, 1)]),
+                out=woven(columns(parts, 2 * i + 1, cols)),
+                in0=rows(w_sb[i][:, :, cols]),
+                in1=woven(columns(parts, 2 * i, cols)),
                 op=ALU.subtract,
             )
 
         def split_first():
             hi_first = keep.tile([P, PACK, P], F32, name="hi_first", align_bytes=64)
-            halves = [slice(0, P // 2), slice(P // 2, P)]
             for cols in halves:
                 nc.vector.tensor_scalar(
                     hi_first[:, :, cols].bitcast(I32),
@@ -150,7 +157,7 @@ def tile_list_tabw_hl_bias_kernel(tc, tab, w, b, offs, out):
                     in1=rows(hi_first[:, :, cols]),
                     op=ALU.subtract,
                 )
-            nc.scalar.copy(out=woven(parts[:, span(0, 1)]), in_=upper_halves(hi_first))
+            nc.scalar.copy(out=woven(parts[:, span(0, 1)]), in_=upper_halves(hi_first[:]))
 
         group_codes = [codes[:, g * P : (g + 1) * P] for g in range(groups)]
 
@@ -212,24 +219,30 @@ def tile_list_tabw_hl_bias_kernel(tc, tab, w, b, offs, out):
             if a == PASSES - 1:
                 finish(m)
 
-        nc.sync.dma_start(offsets[:], offs)
         load_w(0)
-        nc.sync.dma_start(out=bias_rows[spare:P, :], in_=b.rearrange("(m p) -> m p", p=P))
+        nc.sync.dma_start(offsets[:], offs)
         load_scale_rows()
         for i in range(1, len(PIECES)):
             load_w(i)
+            if i == WORDS_AFTER[0]:
+                nc.sync.dma_start(out=bias_rows[spare:P, :], in_=b.rearrange("(m p) -> m p", p=P))
             if i in WORDS_AFTER:
                 load_table(WORDS_AFTER.index(i))
         turned = psum.tile([P, P], F32, name="turned")
         nc.tensor.transpose(turned[:], bias_rows[:], identity[:])
         nc.scalar.copy(out=bias[:], in_=turned[:, spare:P])
         split_first()
-        for i in range(1, len(PIECES)):
+        for cols in halves:
+            take_top(1, cols)
+        for i in range(2, len(PIECES)):
             take_top(i)
 
         waiting = []
         for i in range(last):
-            if i > 0:
+            if i == 1:
+                for cols in halves:
+                    rest(i, cols)
+            elif i > 1:
                 rest(i)
             if i == SCALES_AFTER:
                 gather_scales()
@@ -238,8 +251,13 @@ def tile_list_tabw_hl_bias_kernel(tc, tab, w, b, offs, out):
                 for earlier in waiting:
                     multiply(earlier)
                 waiting.clear()
-            mask(i + 1)
-            quantize_piece(i)
+            if i == 0:
+                mask(1, halves[0])
+                quantize_piece(i)
+                mask(1, halves[1])
+            else:
+                mask(i + 1)
+                quantize_piece(i)
             if i < WORDS_AFTER[PIECES[i][0]]:
                 waiting.append(i)
             else:

@@ -23,9 +23,11 @@ SCALE_ROWS = 4
 HI_MASK_PAIR = -983056
 HI_MASK_F32 = -1048576
 RUN = 2
+SIGN_F32 = -2147483648
 PIECES = [(a, m) for a in range(PASSES) for m in range(TILES - 1)] + [(a, TILES - 1) for a in range(PASSES)]
-SCALES_AFTER = 0
-WORDS_AFTER = (2, 4)
+TURNED = 2
+JOINED = 6
+TABLE_AFTER = (2, 4)
 
 
 def tile_list_tabw_hl_bias_kernel(tc, tab, w, b, offs, out):
@@ -40,14 +42,25 @@ def tile_list_tabw_hl_bias_kernel(tc, tab, w, b, offs, out):
         nc.vector.memset(planes[:, 0 : T // 8], 0)
         nc.gpsimd.memset(planes[:, T // 8 : T // 4], 0)
 
-        groups = 2 * len(PIECES)
         last = len(PIECES) - 1
-        top = keep.tile([P, len(PIECES) * P * PACK], BF16, name="top", align_bytes=64)
-        parts = keep.tile([P, groups * P * PACK], BF16, name="parts", align_bytes=64)
-        codes = keep.tile([P, groups * P], U32, name="codes", align_bytes=64)
-        scales = keep.tile([P, groups * P], U8, name="scales", align_bytes=64)
+        order = []
+        for i in range(len(PIECES)):
+            order.append((i, "hi"))
+            if i == JOINED:
+                order.append((TURNED, "lo"))
+            if i != TURNED:
+                order.append((i, "lo"))
+        place = {group: g for g, group in enumerate(order)}
+        parts = keep.tile([P, len(order) * P * PACK], BF16, name="parts", align_bytes=64)
+        codes = keep.tile([P, len(order) * P], U32, name="codes", align_bytes=64)
+        scales = keep.tile([P, len(order) * P], U8, name="scales", align_bytes=64)
+        top = {
+            i: keep.tile([P, P * PACK], BF16, name="top%d" % i, tag="top%d" % i, align_bytes=64)
+            for i in range(1, len(PIECES))
+            if i != TURNED
+        }
         words = [keep.tile([P, T], I32, name="words%d" % a, align_bytes=64) for a in range(PASSES)]
-        picked = [keep.tile([P, S], U32, name="picked%d" % a, align_bytes=64) for a in range(PASSES)]
+        picked = {}
         picked_scales = keep.tile([P, S], U8, name="picked_scales", align_bytes=64)
         w_sb = []
 
@@ -88,17 +101,27 @@ def tile_list_tabw_hl_bias_kernel(tc, tab, w, b, offs, out):
         for q in range(P // QUADRANT):
             nc.vector.memset(corner[QUADRANT * q : QUADRANT * (q + 1), :], float(QUADRANT * q))
         nc.vector.tensor_tensor_scan(column[:], ones[:], ones[:], 0.0, ALU.mult, ALU.add)
+        unit = keep.tile([P, 1], F32, name="unit", tag="unit", align_bytes=64)
+        nc.vector.memset(unit[:], 1.0)
+        nought = keep.tile([P, 1], F32, name="nought", tag="nought", align_bytes=64)
+        nc.vector.memset(nought[:], 0.0)
         nc.vector.transpose(row[:], column[:, 0:QUADRANT])
         nc.vector.tensor_scalar(identity[:], column[:], corner[:], row[:, 0:1], op0=ALU.subtract, op1=ALU.is_equal)
 
-        shared = {
-            SCALES_AFTER: ("zero", {"bias": zero[:]}),
-            WORDS_AFTER[0]: ("ones", {"scale": ones[:, 0:1]}),
-            WORDS_AFTER[1]: ("column", {"scale": column[:, 0:1]}),
-        }
+        whole = slice(0, P)
+        halves = [slice(0, P // 2), slice(P // 2, P)]
 
-        def span(first, count):
-            return slice(first * P * PACK, (first + count) * P * PACK)
+        late = {}
+
+        def groups_at(g, count, cols=whole):
+            if g in late:
+                tile, g = late[g]
+            else:
+                tile = parts
+            return tile[:, (g * P + cols.start) * PACK : ((g + count - 1) * P + cols.stop) * PACK]
+
+        def part(i, kind, cols=whole):
+            return groups_at(place[(i, kind)], 1, cols)
 
         def woven(view):
             return view.rearrange("p (c i j) -> p c j i", i=RUN, j=PACK)
@@ -109,23 +132,18 @@ def tile_list_tabw_hl_bias_kernel(tc, tab, w, b, offs, out):
         def upper_halves(piece):
             return piece.bitcast(BF16).rearrange("p j (c i e) -> p c j i e", i=RUN, e=2)[:, :, :, :, 1]
 
-        whole = slice(0, P)
-        halves = [slice(0, P // 2), slice(P // 2, P)]
-
-        def columns(tile, group, cols):
-            return tile[:, (group * P + cols.start) * PACK : (group * P + cols.stop) * PACK]
-
-        def take_top(i, cols=whole):
+        def take_top(i, cols=whole, **constant):
+            target = woven(top[i][:, cols.start * PACK : cols.stop * PACK])
             source = upper_halves(w_sb[i][:, :, cols])
-            if i - 1 in shared and cols.start == 0:
-                nc.scalar.activation(woven(columns(top, i, cols)), source, ACT.Identity, **shared[i - 1][1])
+            if constant:
+                nc.scalar.activation(target, source, ACT.Identity, **constant)
             else:
-                nc.scalar.copy(out=woven(columns(top, i, cols)), in_=source)
+                nc.scalar.copy(out=target, in_=source)
 
         def mask(i, cols=whole):
             nc.vector.tensor_scalar(
-                columns(parts, 2 * i, cols).bitcast(I32),
-                columns(top, i, cols).bitcast(I32),
+                part(i, "hi", cols).bitcast(I32),
+                top[i][:, cols.start * PACK : cols.stop * PACK].bitcast(I32),
                 HI_MASK_PAIR,
                 None,
                 op0=ALU.bitwise_and,
@@ -133,9 +151,9 @@ def tile_list_tabw_hl_bias_kernel(tc, tab, w, b, offs, out):
 
         def rest(i, cols=whole):
             nc.vector.tensor_tensor(
-                out=woven(columns(parts, 2 * i + 1, cols)),
+                out=woven(part(i, "lo", cols)),
                 in0=rows(w_sb[i][:, :, cols]),
-                in1=woven(columns(parts, 2 * i, cols)),
+                in1=woven(part(i, "hi", cols)),
                 op=ALU.subtract,
             )
 
@@ -149,36 +167,33 @@ def tile_list_tabw_hl_bias_kernel(tc, tab, w, b, offs, out):
                     None,
                     op0=ALU.bitwise_and,
                 )
-            lo_first = parts[:, span(1, 1)]
             for cols in halves:
                 nc.vector.tensor_tensor(
-                    out=woven(lo_first[:, PACK * cols.start : PACK * cols.stop]),
+                    out=woven(part(0, "lo", cols)),
                     in0=rows(w_sb[0][:, :, cols]),
                     in1=rows(hi_first[:, :, cols]),
                     op=ALU.subtract,
                 )
-            nc.scalar.copy(out=woven(parts[:, span(0, 1)]), in_=upper_halves(hi_first[:]))
+            nc.scalar.copy(out=woven(part(0, "hi")), in_=upper_halves(hi_first[:]))
 
-        group_codes = [codes[:, g * P : (g + 1) * P] for g in range(groups)]
+        group_codes = {group: codes[:, g * P : (g + 1) * P] for group, g in place.items()}
 
-        def quantize(target, first, count):
+        def quantize(group, count=1, tag=None):
+            g = place[group]
+            target = codes[:, g * P : (g + count) * P]
+            if tag is not None:
+                held = keep.tile([P, count * P], U32, name="held%d" % g, tag=tag, align_bytes=64)
+                target = held[:]
+                for c in range(count):
+                    group_codes[order[g + c]] = held[:, c * P : (c + 1) * P]
             nc.vector.quantize_mx(
                 out=target.bitcast(FP8X4),
-                scales=scales[:, first * P : (first + count) * P],
-                in_=parts[:, span(first, count)],
+                scales=scales[:, g * P : (g + count) * P],
+                in_=groups_at(g, count),
             )
 
-        def quantize_piece(i):
-            if i in shared:
-                pair = keep.tile([P, 2 * P], U32, name="pair%d" % i, tag=shared[i][0], align_bytes=64)
-                group_codes[2 * i] = pair[:, 0:P]
-                group_codes[2 * i + 1] = pair[:, P : 2 * P]
-                quantize(pair[:], 2 * i, 2)
-            else:
-                for g in (2 * i, 2 * i + 1):
-                    quantize(group_codes[g], g, 1)
-
-        def gather_words(a):
+        def gather_words(a, tag):
+            picked[a] = keep.tile([P, S], U32, name="picked%d" % a, tag=tag, align_bytes=64)
             nc.vector.tensor_copy(picked[a][:], words[a][:].bitcast(U32).indirect(offsets[:]))
 
         def gather_scales():
@@ -198,12 +213,13 @@ def tile_list_tabw_hl_bias_kernel(tc, tab, w, b, offs, out):
                     nc.scalar.activation(res[:], acc[:, 0:jn], ACT.Identity, bias=bias[:, m : m + 1])
                 nc.sync.dma_start(out=out[m * P : (m + 1) * P, j0 : j0 + jn], in_=res[:])
 
-        def one_pass(g, bank, opens, closes):
-            a = PIECES[g // 2][0]
+        def one_pass(group, bank, opens, closes):
+            a = PIECES[group[0]][0]
+            g = place[group]
             j0, jn, acc = bank
             nc.tensor.matmul_mx(
                 out=acc[:, 0:jn],
-                lhsT=group_codes[g].bitcast(FP8X4),
+                lhsT=group_codes[group].bitcast(FP8X4),
                 lhsT_scale=scales[:, g * P : (g + 1) * P],
                 rhs=picked[a][:, j0 : j0 + jn].bitcast(FP8X4),
                 rhs_scale=picked_scales[SCALE_ROWS * a : P, j0 : j0 + jn],
@@ -211,12 +227,15 @@ def tile_list_tabw_hl_bias_kernel(tc, tab, w, b, offs, out):
                 stop=closes,
             )
 
-        def multiply(i):
-            a, m = PIECES[i]
-            for is_lo in (False, True):
-                for bank in banks[m]:
-                    one_pass(2 * i + is_lo, bank, a == 0 and not is_lo, a == PASSES - 1 and is_lo)
-            if a == PASSES - 1:
+        def multiply(group):
+            a, m = PIECES[group[0]]
+            opens = a == 0 and group[1] == "hi"
+            closes = a == PASSES - 1 and group[1] == "lo"
+            if m == PIECES[TURNED][1]:
+                closes = group == (TURNED, "lo")
+            for bank in banks[m]:
+                one_pass(group, bank, opens, closes)
+            if closes:
                 finish(m)
 
         load_w(0)
@@ -224,50 +243,103 @@ def tile_list_tabw_hl_bias_kernel(tc, tab, w, b, offs, out):
         load_scale_rows()
         for i in range(1, len(PIECES)):
             load_w(i)
-            if i == WORDS_AFTER[0]:
+            if i == TABLE_AFTER[0]:
                 nc.sync.dma_start(out=bias_rows[spare:P, :], in_=b.rearrange("(m p) -> m p", p=P))
-            if i in WORDS_AFTER:
-                load_table(WORDS_AFTER.index(i))
-        turned = psum.tile([P, P], F32, name="turned")
-        nc.tensor.transpose(turned[:], bias_rows[:], identity[:])
-        nc.scalar.copy(out=bias[:], in_=turned[:, spare:P])
-        split_first()
-        for cols in halves:
-            take_top(1, cols)
-        for i in range(2, len(PIECES)):
-            take_top(i)
+            if i in TABLE_AFTER:
+                load_table(TABLE_AFTER.index(i))
 
-        waiting = []
-        for i in range(last):
-            if i == 1:
-                for cols in halves:
-                    rest(i, cols)
-            elif i > 1:
-                rest(i)
-            if i == SCALES_AFTER:
-                gather_scales()
-            if i in WORDS_AFTER:
-                gather_words(WORDS_AFTER.index(i))
-                for earlier in waiting:
-                    multiply(earlier)
-                waiting.clear()
-            if i == 0:
-                mask(1, halves[0])
-                quantize_piece(i)
-                mask(1, halves[1])
-            else:
-                mask(i + 1)
-                quantize_piece(i)
-            if i < WORDS_AFTER[PIECES[i][0]]:
-                waiting.append(i)
-            else:
-                multiply(i)
+        summed = psum.tile([P, PACK, P], F32, name="summed")
+        for j in range(PACK):
+            nc.tensor.matmul(summed[:, j, :], w_sb[TURNED][:, j, :], identity[:], start=j == 0, stop=False, is_transpose=True)
+        turned_bias = psum.tile([P, P], F32, name="turned_bias")
+        nc.tensor.transpose(turned_bias[:], bias_rows[:], identity[:])
+
+        split_first()
+        gather_scales()
+        take_top(1, halves[0], bias=zero[:])
+        take_top(1, halves[1])
+        nc.scalar.copy(out=bias[:], in_=turned_bias[:, spare:P])
+        mask(1, halves[0])
+        quantize((0, "hi"), 2, "zero")
+        mask(1, halves[1])
+        minus_hi = keep.tile([P, PACK, P], F32, name="minus_hi", align_bytes=64)
+        nc.vector.tensor_scalar(
+            minus_hi[:].bitcast(I32),
+            w_sb[TURNED][:].bitcast(I32),
+            HI_MASK_F32,
+            SIGN_F32,
+            op0=ALU.bitwise_and,
+            op1=ALU.bitwise_xor,
+        )
+        for j in range(PACK):
+            nc.tensor.matmul(summed[:, j, :], minus_hi[:, j, :], identity[:], start=False, stop=j == PACK - 1, is_transpose=True)
+        nc.scalar.activation(woven(part(TURNED, "hi")), upper_halves(minus_hi[:]), ACT.Identity, scale=-1.0)
+        for cols in halves:
+            rest(1, cols)
+        gather_words(0, "picked0")
+        quantize((1, "hi"))
+        for group in [(0, "hi"), (0, "lo"), (1, "hi")]:
+            multiply(group)
+        take_top(3, halves[0], scale=ones[:, 0:1])
+        take_top(3, halves[1])
+        take_top(4)
+        mask(3, halves[0])
+        quantize((1, "lo"), 2, "ones")
+        multiply((1, "lo"))
+        multiply((TURNED, "hi"))
+        mask(3, halves[1])
+        rounded = keep.tile([P, P * PACK], BF16, name="rounded", tag="top3", align_bytes=64)
+        nc.scalar.activation(
+            rounded[:].rearrange("n (u p e) -> n u p e", u=2, e=2),
+            summed[:].rearrange("n (u e) p -> n u p e", e=2),
+            ACT.Identity,
+            scale=unit[:],
+        )
+        back = psum.tile([P, 2, P], F32, name="back")
+        for u in range(2):
+            nc.tensor.transpose(back[:, u, :], rounded[:].bitcast(F32)[:, u * P : (u + 1) * P], identity[:])
+        for cols in halves:
+            rest(3, cols)
+        mask(4)
+        quantize((3, "hi"))
+        quantize((3, "lo"))
+        take_top(5, scale=column[:, 0:1], bias=nought[:])
+        take_top(6)
+        joined = keep.tile([P, P * PACK], BF16, name="joined", tag="nought", align_bytes=64)
+        late[place[(TURNED, "lo")]] = (joined, 0)
+        nc.scalar.copy(
+            out=part(TURNED, "lo").bitcast(F32).rearrange("p (n u) -> p n u", u=2),
+            in_=back[:].rearrange("p u n -> p n u"),
+        )
+        take_top(7)
+        rest(4)
+        gather_words(1, "unit")
+        mask(5)
+        multiply((3, "hi"))
+        multiply((3, "lo"))
+        quantize((4, "hi"), 2, "column")
+        multiply((4, "hi"))
+        multiply((4, "lo"))
+        rest(5)
+        mask(6)
+        quantize((5, "hi"))
+        quantize((5, "lo"))
+        quantize((TURNED, "lo"))
+        multiply((5, "hi"))
+        multiply((5, "lo"))
+        multiply((TURNED, "lo"))
+        rest(6)
+        mask(7)
+        quantize((6, "hi"))
+        quantize((6, "lo"))
+        multiply((6, "hi"))
+        multiply((6, "lo"))
         rest(last)
-        quantize_piece(last)
-        hi, lo = 2 * last, 2 * last + 1
+        quantize((last, "hi"))
+        quantize((last, "lo"))
         first_bank, second_bank = banks[TILES - 1]
-        one_pass(hi, first_bank, False, False)
-        one_pass(lo, first_bank, False, True)
-        one_pass(lo, second_bank, False, False)
-        one_pass(hi, second_bank, False, True)
+        one_pass((last, "hi"), first_bank, False, False)
+        one_pass((last, "lo"), first_bank, False, True)
+        one_pass((last, "lo"), second_bank, False, False)
+        one_pass((last, "hi"), second_bank, False, True)
         finish(TILES - 1)

@@ -26,6 +26,7 @@ RUN = 2
 SIGN_F32 = -2147483648
 PIECES = [(a, m) for a in range(PASSES) for m in range(TILES - 1)] + [(a, TILES - 1) for a in range(PASSES)]
 TURNED = 2
+FIRST = 0
 JOINED = 6
 TABLE_AFTER = (2, 4)
 
@@ -45,10 +46,12 @@ def tile_list_tabw_hl_bias_kernel(tc, tab, w, b, offs, out):
         last = len(PIECES) - 1
         order = []
         for i in range(len(PIECES)):
+            if i == 4:
+                order.append((FIRST, "lo"))
             order.append((i, "hi"))
             if i == JOINED:
                 order.append((TURNED, "lo"))
-            if i != TURNED:
+            if i not in (FIRST, TURNED):
                 order.append((i, "lo"))
         place = {group: g for g, group in enumerate(order)}
         parts = keep.tile([P, len(order) * P * PACK], BF16, name="parts", align_bytes=64)
@@ -103,6 +106,12 @@ def tile_list_tabw_hl_bias_kernel(tc, tab, w, b, offs, out):
         nc.vector.tensor_tensor_scan(column[:], ones[:], ones[:], 0.0, ALU.mult, ALU.add)
         unit = keep.tile([P, 1], F32, name="unit", tag="unit", align_bytes=64)
         nc.vector.memset(unit[:], 1.0)
+        held_two = keep.tile([P, 1], F32, name="held_two", tag="held_two", align_bytes=64)
+        nc.vector.memset(held_two[:], 1.0)
+        held_one = keep.tile([P, 1], F32, name="held_one", tag="held_one", align_bytes=64)
+        nc.vector.memset(held_one[:], 1.0)
+        held_four = keep.tile([P, 1], F32, name="held_four", tag="held_four", align_bytes=64)
+        nc.vector.memset(held_four[:], 1.0)
         nought = keep.tile([P, 1], F32, name="nought", tag="nought", align_bytes=64)
         nc.vector.memset(nought[:], 0.0)
         nc.vector.transpose(row[:], column[:, 0:QUADRANT])
@@ -157,24 +166,47 @@ def tile_list_tabw_hl_bias_kernel(tc, tab, w, b, offs, out):
                 op=ALU.subtract,
             )
 
-        def split_first():
-            hi_first = keep.tile([P, PACK, P], F32, name="hi_first", align_bytes=64)
-            for cols in halves:
-                nc.vector.tensor_scalar(
-                    hi_first[:, :, cols].bitcast(I32),
-                    w_sb[0][:, :, cols].bitcast(I32),
-                    HI_MASK_F32,
-                    None,
-                    op0=ALU.bitwise_and,
+        def add_turned(bank, source, opens):
+            for j in range(PACK):
+                nc.tensor.matmul(
+                    bank[:, j, :],
+                    source[:, j, :],
+                    identity[:],
+                    start=opens and j == 0,
+                    stop=not opens and j == PACK - 1,
+                    is_transpose=True,
                 )
-            for cols in halves:
-                nc.vector.tensor_tensor(
-                    out=woven(part(0, "lo", cols)),
-                    in0=rows(w_sb[0][:, :, cols]),
-                    in1=rows(hi_first[:, :, cols]),
-                    op=ALU.subtract,
-                )
-            nc.scalar.copy(out=woven(part(0, "hi")), in_=upper_halves(hi_first[:]))
+
+        def negated_hi(i, tag):
+            tile = keep.tile([P, PACK, P], F32, name="minus_hi%d" % i, tag=tag, align_bytes=64)
+            nc.vector.tensor_scalar(
+                tile[:].bitcast(I32),
+                w_sb[i][:].bitcast(I32),
+                HI_MASK_F32,
+                SIGN_F32,
+                op0=ALU.bitwise_and,
+                op1=ALU.bitwise_xor,
+            )
+            add_turned(summed[i], tile, False)
+            nc.scalar.activation(woven(part(i, "hi")), upper_halves(tile[:]), ACT.Identity, scale=-1.0)
+
+        def turn_back(i, tag, bank_tag, **constant):
+            rounded = keep.tile([P, P * PACK], BF16, name="rounded%d" % i, tag=tag, align_bytes=64)
+            nc.scalar.activation(
+                rounded[:].rearrange("n (u p e) -> n u p e", u=2, e=2),
+                summed[i][:].rearrange("n (u e) p -> n u p e", e=2),
+                ACT.Identity,
+                **constant
+            )
+            back[i] = psum.tile([P, 2, P], F32, name="back%d" % i, tag=bank_tag)
+            for u in range(2):
+                nc.tensor.transpose(back[i][:, u, :], rounded[:].bitcast(F32)[:, u * P : (u + 1) * P], identity[:])
+
+        def take_words(i):
+            nc.scalar.copy(
+                out=part(i, "lo").bitcast(F32).rearrange("p (n u) -> p n u", u=2),
+                in_=back[i][:].rearrange("p u n -> p n u"),
+            )
 
         group_codes = {group: codes[:, g * P : (g + 1) * P] for group, g in place.items()}
 
@@ -198,11 +230,6 @@ def tile_list_tabw_hl_bias_kernel(tc, tab, w, b, offs, out):
 
         def gather_scales():
             nc.vector.tensor_copy(picked_scales[:], planes[:].bitcast(U8).indirect(offsets[:]))
-
-        banks = []
-        for m in range(TILES):
-            ranges = [(0, S)] if m < TILES - 1 else [(0, S // 2), (S // 2, S // 2)]
-            banks.append([(j0, jn, psum.tile([P, S], F32, name="acc%d_%d" % (m, j0))) for j0, jn in ranges])
 
         def finish(m):
             for j0, jn, acc in banks[m]:
@@ -231,8 +258,8 @@ def tile_list_tabw_hl_bias_kernel(tc, tab, w, b, offs, out):
             a, m = PIECES[group[0]]
             opens = a == 0 and group[1] == "hi"
             closes = a == PASSES - 1 and group[1] == "lo"
-            if m == PIECES[TURNED][1]:
-                closes = group == (TURNED, "lo")
+            if m in (PIECES[FIRST][1], PIECES[TURNED][1]):
+                closes = a == 0 and group[1] == "lo"
             for bank in banks[m]:
                 one_pass(group, bank, opens, closes)
             if closes:
@@ -248,56 +275,46 @@ def tile_list_tabw_hl_bias_kernel(tc, tab, w, b, offs, out):
             if i in TABLE_AFTER:
                 load_table(TABLE_AFTER.index(i))
 
-        summed = psum.tile([P, PACK, P], F32, name="summed")
-        for j in range(PACK):
-            nc.tensor.matmul(summed[:, j, :], w_sb[TURNED][:, j, :], identity[:], start=j == 0, stop=False, is_transpose=True)
-        turned_bias = psum.tile([P, P], F32, name="turned_bias")
-        nc.tensor.transpose(turned_bias[:], bias_rows[:], identity[:])
-
-        split_first()
+        summed = {i: psum.tile([P, PACK, P], F32, name="summed%d" % i, tag="summed%d" % i) for i in (FIRST, TURNED)}
+        back = {}
+        add_turned(summed[FIRST], w_sb[FIRST], True)
+        negated_hi(FIRST, "minus_hi0")
         gather_scales()
-        take_top(1, halves[0], bias=zero[:])
-        take_top(1, halves[1])
+        take_top(1, halves[0], bias=zero[:], scale=held_two[:])
+        take_top(1, halves[1], scale=held_one[:])
+        turn_back(FIRST, "held_one", "back0")
+        add_turned(summed[TURNED], w_sb[TURNED], True)
+        turned_bias = psum.tile([P, P], F32, name="turned_bias", tag="acc3_256")
+        nc.tensor.transpose(turned_bias[:], bias_rows[:], identity[:])
         nc.scalar.copy(out=bias[:], in_=turned_bias[:, spare:P])
+        banks = []
+        for m in range(TILES):
+            ranges = [(0, S)] if m < TILES - 1 else [(0, S // 2), (S // 2, S // 2)]
+            banks.append([(j0, jn, psum.tile([P, S], F32, name="acc%d_%d" % (m, j0), tag="acc%d_%d" % (m, j0))) for j0, jn in ranges])
+
         mask(1, halves[0])
-        quantize((0, "hi"), 2, "zero")
+        quantize((0, "hi"), 1, "zero")
+        negated_hi(TURNED, "held_two")
         mask(1, halves[1])
-        minus_hi = keep.tile([P, PACK, P], F32, name="minus_hi", align_bytes=64)
-        nc.vector.tensor_scalar(
-            minus_hi[:].bitcast(I32),
-            w_sb[TURNED][:].bitcast(I32),
-            HI_MASK_F32,
-            SIGN_F32,
-            op0=ALU.bitwise_and,
-            op1=ALU.bitwise_xor,
-        )
-        for j in range(PACK):
-            nc.tensor.matmul(summed[:, j, :], minus_hi[:, j, :], identity[:], start=False, stop=j == PACK - 1, is_transpose=True)
-        nc.scalar.activation(woven(part(TURNED, "hi")), upper_halves(minus_hi[:]), ACT.Identity, scale=-1.0)
         for cols in halves:
             rest(1, cols)
         gather_words(0, "picked0")
         quantize((1, "hi"))
-        for group in [(0, "hi"), (0, "lo"), (1, "hi")]:
+        for group in [(0, "hi"), (1, "hi")]:
             multiply(group)
         take_top(3, halves[0], scale=ones[:, 0:1])
         take_top(3, halves[1])
-        take_top(4)
+        take_top(4, scale=held_four[:])
         mask(3, halves[0])
         quantize((1, "lo"), 2, "ones")
         multiply((1, "lo"))
         multiply((TURNED, "hi"))
         mask(3, halves[1])
-        rounded = keep.tile([P, P * PACK], BF16, name="rounded", tag="top3", align_bytes=64)
-        nc.scalar.activation(
-            rounded[:].rearrange("n (u p e) -> n u p e", u=2, e=2),
-            summed[:].rearrange("n (u e) p -> n u p e", e=2),
-            ACT.Identity,
-            scale=unit[:],
-        )
-        back = psum.tile([P, 2, P], F32, name="back")
-        for u in range(2):
-            nc.tensor.transpose(back[:, u, :], rounded[:].bitcast(F32)[:, u * P : (u + 1) * P], identity[:])
+        turn_back(TURNED, "top3", "summed0", scale=unit[:])
+        trio = keep.tile([P, 3 * P * PACK], BF16, name="trio", tag="held_four", align_bytes=64)
+        for c, group in enumerate([(FIRST, "lo"), (4, "hi"), (4, "lo")]):
+            late[place[group]] = (trio, c)
+        take_words(FIRST)
         for cols in halves:
             rest(3, cols)
         mask(4)
@@ -307,17 +324,15 @@ def tile_list_tabw_hl_bias_kernel(tc, tab, w, b, offs, out):
         take_top(6)
         joined = keep.tile([P, P * PACK], BF16, name="joined", tag="nought", align_bytes=64)
         late[place[(TURNED, "lo")]] = (joined, 0)
-        nc.scalar.copy(
-            out=part(TURNED, "lo").bitcast(F32).rearrange("p (n u) -> p n u", u=2),
-            in_=back[:].rearrange("p u n -> p n u"),
-        )
+        take_words(TURNED)
         take_top(7)
         rest(4)
         gather_words(1, "unit")
         mask(5)
         multiply((3, "hi"))
         multiply((3, "lo"))
-        quantize((4, "hi"), 2, "column")
+        quantize((FIRST, "lo"), 3, "column")
+        multiply((FIRST, "lo"))
         multiply((4, "hi"))
         multiply((4, "lo"))
         rest(5)

import concourse.mybir as mybir

K, M, T, S = 1024, 512, 1024, 512
FLOPS = 2 * 2 * K * M * S

F32 = mybir.dt.float32
BF16 = mybir.dt.bfloat16
I32 = mybir.dt.int32
U32 = mybir.dt.uint32
U16 = mybir.dt.uint16
U8 = mybir.dt.uint8
FP8X4 = mybir.dt.float8_e4m3fn_x4
ALU = mybir.AluOpType
ACT = mybir.ActivationFunctionType

P = 128
PACK = 4
K_PASS = P * PACK
PASSES = K // K_PASS
TILES = M // P
QUADRANT = 32
SCALE_ROWS = 4
HI_MASK_PAIR = -983056
HI_MASK_F32 = -1048576
RUN = 2
SIGN_F32 = -2147483648
PIECES = [(a, m) for a in range(PASSES) for m in range(TILES - 1)] + [(a, TILES - 1) for a in range(PASSES)]
TURNED = 2
FIRST = 0
JOINED = 6
TABLE_AFTER = (2, 4)


def tile_list_tabw_hl_bias_kernel(tc, tab, w, b, offs, out):
    nc = tc.nc
    with (
        tc.tile_pool(name="keep", bufs=1) as keep,
        tc.psum_pool(name="psum", bufs=1) as psum,
    ):
        offsets = keep.tile([P, S // 16], U16, name="offsets")
        planes = keep.tile([P, T // 4], I32, name="planes", align_bytes=64)
        bias = keep.tile([P, TILES], F32, name="bias")
        nc.vector.memset(planes[:, 0 : T // 8], 0)
        nc.gpsimd.memset(planes[:, T // 8 : T // 4], 0)

        last = len(PIECES) - 1
        order = []
        for i in range(len(PIECES)):
            if i == 4:
                order.append((FIRST, "lo"))
            order.append((i, "hi"))
            if i == JOINED:
                order.append((TURNED, "lo"))
            if i not in (FIRST, TURNED):
                order.append((i, "lo"))
        place = {group: g for g, group in enumerate(order)}
        parts = keep.tile([P, len(order) * P * PACK], BF16, name="parts", align_bytes=64)
        codes = keep.tile([P, len(order) * P], U32, name="codes", align_bytes=64)
        scales = keep.tile([P, len(order) * P], U8, name="scales", align_bytes=64)
        top = {
            i: keep.tile([P, P * PACK], BF16, name="top%d" % i, tag="top%d" % i, align_bytes=64)
            for i in range(1, len(PIECES))
            if i != TURNED
        }
        words = [keep.tile([P, T], I32, name="words%d" % a, align_bytes=64) for a in range(PASSES)]
        picked = {}
        picked_scales = keep.tile([P, S], U8, name="picked_scales", align_bytes=64)
        w_sb = []

        def load_w(i):
            a, m = PIECES[i]
            piece = keep.tile([P, PACK, P], F32, name="w%d_%d" % (a, m), align_bytes=64)
            nc.sync.dma_start(
                out=piece[:],
                in_=w[a * K_PASS : (a + 1) * K_PASS, m * P : (m + 1) * P].rearrange("(p j) n -> p j n", j=PACK),
            )
            w_sb.append(piece)

        def load_table(a):
            nc.sync.dma_start(
                out=words[a][:],
                in_=tab[a, 0 : PACK * P * T].rearrange("(p x) -> p x", p=P).bitcast(I32),
            )

        def load_scale_rows():
            for q in range(P // QUADRANT):
                first = PACK * P * T + SCALE_ROWS * q * T
                nc.sync.dma_start(
                    out=planes[QUADRANT * q : QUADRANT * q + PASSES * SCALE_ROWS, :],
                    in_=tab[:, first : first + SCALE_ROWS * T].rearrange("a (r t) -> a r t", r=SCALE_ROWS).bitcast(I32),
                )

        bias_rows = keep.tile([P, P], F32, name="bias_rows", align_bytes=64)
        identity = keep.tile([P, P], F32, name="identity", align_bytes=64)
        spare = P - TILES
        zero = keep.tile([P, 1], F32, name="zero", tag="zero", align_bytes=64)
        nc.vector.memset(zero[:], 0.0)
        nc.scalar.activation(bias_rows[0:spare, :], zero[0:spare, :].to_broadcast([spare, P]), ACT.Identity)
        ones = keep.tile([P, P], F32, name="ones", tag="ones", align_bytes=64)
        column = keep.tile([P, P], F32, name="column", tag="column", align_bytes=64)
        corner = keep.tile([P, 1], F32, name="corner")
        row = keep.tile([P, QUADRANT], F32, name="row", align_bytes=64)
        nc.vector.memset(ones[:], 1.0)
        for q in range(P // QUADRANT):
            nc.vector.memset(corner[QUADRANT * q : QUADRANT * (q + 1), :], float(QUADRANT * q))
        nc.vector.tensor_tensor_scan(column[:], ones[:], ones[:], 0.0, ALU.mult, ALU.add)
        unit = keep.tile([P, 1], F32, name="unit", tag="unit", align_bytes=64)
        nc.vector.memset(unit[:], 1.0)
        held_two = keep.tile([P, 1], F32, name="held_two", tag="held_two", align_bytes=64)
        nc.vector.memset(held_two[:], 1.0)
        held_one = keep.tile([P, 1], F32, name="held_one", tag="held_one", align_bytes=64)
        nc.vector.memset(held_one[:], 1.0)
        held_four = keep.tile([P, 1], F32, name="held_four", tag="held_four", align_bytes=64)
        nc.vector.memset(held_four[:], 1.0)
        nought = keep.tile([P, 1], F32, name="nought", tag="nought", align_bytes=64)
        nc.vector.memset(nought[:], 0.0)
        nc.vector.transpose(row[:], column[:, 0:QUADRANT])
        nc.vector.tensor_scalar(identity[:], column[:], corner[:], row[:, 0:1], op0=ALU.subtract, op1=ALU.is_equal)

        whole = slice(0, P)
        halves = [slice(0, P // 2), slice(P // 2, P)]

        late = {}

        def groups_at(g, count, cols=whole):
            if g in late:
                tile, g = late[g]
            else:
                tile = parts
            return tile[:, (g * P + cols.start) * PACK : ((g + count - 1) * P + cols.stop) * PACK]

        def part(i, kind, cols=whole):
            return groups_at(place[(i, kind)], 1, cols)

        def woven(view):
            return view.rearrange("p (c i j) -> p c j i", i=RUN, j=PACK)

        def rows(view):
            return view.rearrange("p j (c i) -> p c j i", i=RUN)

        def upper_halves(piece):
            return piece.bitcast(BF16).rearrange("p j (c i e) -> p c j i e", i=RUN, e=2)[:, :, :, :, 1]

        def take_top(i, cols=whole, **constant):
            target = woven(top[i][:, cols.start * PACK : cols.stop * PACK])
            source = upper_halves(w_sb[i][:, :, cols])
            if constant:
                nc.scalar.activation(target, source, ACT.Identity, **constant)
            else:
                nc.scalar.copy(out=target, in_=source)

        def mask(i, cols=whole):
            nc.vector.tensor_scalar(
                part(i, "hi", cols).bitcast(I32),
                top[i][:, cols.start * PACK : cols.stop * PACK].bitcast(I32),
                HI_MASK_PAIR,
                None,
                op0=ALU.bitwise_and,
            )

        def rest(i, cols=whole):
            nc.vector.tensor_tensor(
                out=woven(part(i, "lo", cols)),
                in0=rows(w_sb[i][:, :, cols]),
                in1=woven(part(i, "hi", cols)),
                op=ALU.subtract,
            )

        def add_turned(bank, source, opens):
            for j in range(PACK):
                nc.tensor.matmul(
                    bank[:, j, :],
                    source[:, j, :],
                    identity[:],
                    start=opens and j == 0,
                    stop=not opens and j == PACK - 1,
                    is_transpose=True,
                )

        def negated_hi(i, tag):
            tile = keep.tile([P, PACK, P], F32, name="minus_hi%d" % i, tag=tag, align_bytes=64)
            nc.vector.tensor_scalar(
                tile[:].bitcast(I32),
                w_sb[i][:].bitcast(I32),
                HI_MASK_F32,
                SIGN_F32,
                op0=ALU.bitwise_and,
                op1=ALU.bitwise_xor,
            )
            add_turned(summed[i], tile, False)
            nc.scalar.activation(woven(part(i, "hi")), upper_halves(tile[:]), ACT.Identity, scale=-1.0)

        def turn_back(i, tag, bank_tag, **constant):
            rounded = keep.tile([P, P * PACK], BF16, name="rounded%d" % i, tag=tag, align_bytes=64)
            nc.scalar.activation(
                rounded[:].rearrange("n (u p e) -> n u p e", u=2, e=2),
                summed[i][:].rearrange("n (u e) p -> n u p e", e=2),
                ACT.Identity,
                **constant
            )
            back[i] = psum.tile([P, 2, P], F32, name="back%d" % i, tag=bank_tag)
            for u in range(2):
                nc.tensor.transpose(back[i][:, u, :], rounded[:].bitcast(F32)[:, u * P : (u + 1) * P], identity[:])

        def take_words(i):
            nc.scalar.copy(
                out=part(i, "lo").bitcast(F32).rearrange("p (n u) -> p n u", u=2),
                in_=back[i][:].rearrange("p u n -> p n u"),
            )

        group_codes = {group: codes[:, g * P : (g + 1) * P] for group, g in place.items()}

        def quantize(group, count=1, tag=None):
            g = place[group]
            target = codes[:, g * P : (g + count) * P]
            if tag is not None:
                held = keep.tile([P, count * P], U32, name="held%d" % g, tag=tag, align_bytes=64)
                target = held[:]
                for c in range(count):
                    group_codes[order[g + c]] = held[:, c * P : (c + 1) * P]
            nc.vector.quantize_mx(
                out=target.bitcast(FP8X4),
                scales=scales[:, g * P : (g + count) * P],
                in_=groups_at(g, count),
            )

        def gather_words(a, tag):
            picked[a] = keep.tile([P, S], U32, name="picked%d" % a, tag=tag, align_bytes=64)
            nc.vector.tensor_copy(picked[a][:], words[a][:].bitcast(U32).indirect(offsets[:]))

        def gather_scales():
            nc.vector.tensor_copy(picked_scales[:], planes[:].bitcast(U8).indirect(offsets[:]))

        def finish(m):
            for j0, jn, acc in banks[m]:
                res = keep.tile([P, jn], F32, name="res%d_%d" % (m, j0), align_bytes=64)
                if m == TILES - 1 and j0 == 0:
                    nc.vector.tensor_scalar(res[:], acc[:, 0:jn], bias[:, m : m + 1], None, op0=ALU.add)
                else:
                    nc.scalar.activation(res[:], acc[:, 0:jn], ACT.Identity, bias=bias[:, m : m + 1])
                nc.sync.dma_start(out=out[m * P : (m + 1) * P, j0 : j0 + jn], in_=res[:])

        def one_pass(group, bank, opens, closes):
            a = PIECES[group[0]][0]
            g = place[group]
            j0, jn, acc = bank
            nc.tensor.matmul_mx(
                out=acc[:, 0:jn],
                lhsT=group_codes[group].bitcast(FP8X4),
                lhsT_scale=scales[:, g * P : (g + 1) * P],
                rhs=picked[a][:, j0 : j0 + jn].bitcast(FP8X4),
                rhs_scale=picked_scales[SCALE_ROWS * a : P, j0 : j0 + jn],
                start=opens,
                stop=closes,
            )

        def multiply(group):
            a, m = PIECES[group[0]]
            opens = a == 0 and group[1] == "hi"
            closes = a == PASSES - 1 and group[1] == "lo"
            if m in (PIECES[FIRST][1], PIECES[TURNED][1]):
                closes = a == 0 and group[1] == "lo"
            for bank in banks[m]:
                one_pass(group, bank, opens, closes)
            if closes:
                finish(m)

        load_w(0)
        nc.sync.dma_start(offsets[:], offs)
        load_scale_rows()
        for i in range(1, len(PIECES)):
            load_w(i)
            if i == TABLE_AFTER[0]:
                nc.sync.dma_start(out=bias_rows[spare:P, :], in_=b.rearrange("(m p) -> m p", p=P))
            if i in TABLE_AFTER:
                load_table(TABLE_AFTER.index(i))

        summed = {i: psum.tile([P, PACK, P], F32, name="summed%d" % i, tag="summed%d" % i) for i in (FIRST, TURNED)}
        back = {}
        add_turned(summed[FIRST], w_sb[FIRST], True)
        negated_hi(FIRST, "minus_hi0")
        gather_scales()
        take_top(1, halves[0], bias=zero[:], scale=held_two[:])
        take_top(1, halves[1], scale=held_one[:])
        turn_back(FIRST, "held_one", "back0")
        add_turned(summed[TURNED], w_sb[TURNED], True)
        turned_bias = psum.tile([P, P], F32, name="turned_bias", tag="acc3_256")
        nc.tensor.transpose(turned_bias[:], bias_rows[:], identity[:])
        nc.scalar.copy(out=bias[:], in_=turned_bias[:, spare:P])
        banks = []
        for m in range(TILES):
            ranges = [(0, S)] if m < TILES - 1 else [(0, S // 2), (S // 2, S // 2)]
            banks.append([(j0, jn, psum.tile([P, S], F32, name="acc%d_%d" % (m, j0), tag="acc%d_%d" % (m, j0))) for j0, jn in ranges])

        mask(1, halves[0])
        quantize((0, "hi"), 1, "zero")
        negated_hi(TURNED, "held_two")
        mask(1, halves[1])
        for cols in halves:
            rest(1, cols)
        gather_words(0, "picked0")
        quantize((1, "hi"))
        for group in [(0, "hi"), (1, "hi")]:
            multiply(group)
        take_top(3, halves[0], scale=ones[:, 0:1])
        take_top(3, halves[1])
        take_top(4, scale=held_four[:])
        mask(3, halves[0])
        quantize((1, "lo"), 2, "ones")
        multiply((1, "lo"))
        multiply((TURNED, "hi"))
        mask(3, halves[1])
        turn_back(TURNED, "top3", "summed0", scale=unit[:])
        trio = keep.tile([P, 3 * P * PACK], BF16, name="trio", tag="held_four", align_bytes=64)
        for c, group in enumerate([(FIRST, "lo"), (4, "hi"), (4, "lo")]):
            late[place[group]] = (trio, c)
        take_words(FIRST)
        for cols in halves:
            rest(3, cols)
        mask(4)
        quantize((3, "hi"))
        quantize((3, "lo"))
        take_top(5, scale=column[:, 0:1], bias=nought[:])
        take_top(6)
        joined = keep.tile([P, P * PACK], BF16, name="joined", tag="nought", align_bytes=64)
        late[place[(TURNED, "lo")]] = (joined, 0)
        take_words(TURNED)
        take_top(7)
        rest(4)
        gather_words(1, "unit")
        mask(5)
        multiply((3, "hi"))
        multiply((3, "lo"))
        quantize((FIRST, "lo"), 3, "column")
        multiply((FIRST, "lo"))
        multiply((4, "hi"))
        multiply((4, "lo"))
        rest(5)
        mask(6)
        quantize((5, "hi"))
        quantize((5, "lo"))
        quantize((TURNED, "lo"))
        multiply((5, "hi"))
        multiply((5, "lo"))
        multiply((TURNED, "lo"))
        rest(6)
        mask(7)
        quantize((6, "hi"))
        quantize((6, "lo"))
        multiply((6, "hi"))
        multiply((6, "lo"))
        rest(last)
        quantize((last, "hi"))
        quantize((last, "lo"))
        first_bank, second_bank = banks[TILES - 1]
        one_pass((last, "hi"), first_bank, False, False)
        one_pass((last, "lo"), first_bank, False, True)
        one_pass((last, "lo"), second_bank, False, False)
        one_pass((last, "hi"), second_bank, False, True)
        finish(TILES - 1)
